import numpy as np
import ml_dtypes


def mxq(x, axis, fmt="e4m3"):
    dtype, down = {"e4m3": (ml_dtypes.float8_e4m3fn, 7), "e5m2": (ml_dtypes.float8_e5m2, 14)}[fmt]
    v = np.moveaxis(np.asarray(x, np.float32).astype(ml_dtypes.bfloat16).astype(np.float64), axis, -1)
    blocks = v.reshape(v.shape[:-1] + (-1, 32))
    amax = np.abs(blocks).max(-1, keepdims=True)
    byte = np.maximum(np.where(amax > 0, np.frexp(amax)[1] - 1 + 127, 0) - down, 1)
    scale = np.exp2(byte - 127.0)
    codes = (blocks / scale).astype(np.float32).astype(dtype).astype(np.float64)
    return np.moveaxis((codes * scale).reshape(v.shape), -1, axis)


WIDE = False


def mx_kscale(k):
    if not WIDE:
        return np.ones(k)
    levels = np.array([10, -10, 5, -5, 0])
    if k % 512:
        return np.exp2(np.random.permutation(np.resize(levels, k // 32))).repeat(32)
    a = np.empty((k // 512, 16))
    for p in range(k // 512):
        a[p, :8] = np.random.permutation(np.resize(levels, 8))
        for g in range(8):
            far = levels[np.abs(levels - a[p, g]) >= 10]
            a[p, g + 8] = far[np.random.randint(len(far))]
    return np.exp2(a.ravel()).repeat(32)


def f64(x):
    return np.asarray(x).astype(np.float64)


def striped(idx):
    return np.tile(idx.reshape(-1, 16).T, (8, 1)).astype(np.uint16)


def unstriped(offs):
    return offs[:16].T.reshape(-1).astype(np.int64)


E2M1 = np.array([0.0, 0.5, 1.0, 1.5, 2.0, 3.0, 4.0, 6.0, -0.0, -0.5, -1.0, -1.5, -2.0, -3.0, -4.0, -6.0])


def pack_weight(w, fmt):
    k, n = w.shape
    w = f64(np.asarray(w, np.float32).astype(ml_dtypes.bfloat16)).reshape(k // 32, 32, n)
    amax = np.abs(w).max(1)
    if fmt == "e4m3":
        byte = np.frexp(amax)[1] - 1 + 127 - 7
    else:
        mant, ex = np.frexp(amax / 6.0)
        byte = np.where(mant > 0.5, ex, ex - 1) + 127
    byte = np.clip(np.where(amax > 0, byte, 1), 1, 254)
    scaled = (w * np.exp2(127.0 - byte)[:, None, :]).reshape(k, n).astype(np.float32)
    by_word = np.ascontiguousarray(scaled.reshape(k // 512, 128, 4, n).transpose(0, 1, 3, 2))
    if fmt == "e4m3":
        words = by_word.astype(ml_dtypes.float8_e4m3fn).view(np.uint8)
    else:
        c = by_word.astype(ml_dtypes.float4_e2m1fn).view(np.uint8) & 0xF
        words = (c[..., 0::2] | (c[..., 1::2] << 4)).reshape(k // 512, 128, 2 * n)
    return np.ascontiguousarray(words), np.ascontiguousarray(byte.astype(np.uint8).reshape(k // 512, 16, n))


def unpack_weight(words, scales, fmt):
    g, _, n = scales.shape
    words = np.ascontiguousarray(words).reshape(g, 128, n, -1)
    if fmt == "e4m3":
        vals = words.view(ml_dtypes.float8_e4m3fn).astype(np.float64)
    else:
        nib = np.empty((g, 128, n, 4), np.uint8)
        nib[..., 0::2] = words & 0xF
        nib[..., 1::2] = words >> 4
        vals = E2M1[nib]
    vals = vals * np.repeat(np.exp2(scales.astype(np.float64) - 127.0), 8, axis=1)[..., None]
    return vals.transpose(0, 1, 3, 2).reshape(g * 512, n)


def gelu(v):
    return 0.5 * v * (1.0 + np.tanh(np.sqrt(2.0 / np.pi) * (v + 0.044715 * v**3)))


K, T, S, H, N = 1024, 2048, 1024, 1024, 512

def setup_inputs():
    n = np.random.standard_normal
    s = mx_kscale(K)[:, None]
    u = mx_kscale(H)[:, None]
    tab_words, tab_scales = pack_weight(n((K, T)) * s, "e4m3")
    offs = striped(np.random.permutation(T)[:S])
    w1 = (n((K, H)) / np.sqrt(K) / s * u.T).astype(np.float32)
    wg_words, wg_scales = pack_weight(1.5 * n((K, H)) / np.sqrt(K) / s, "e2m1")
    wo_words, wo_scales = pack_weight(2.0 * n((H, N)) / np.sqrt(H) / u, "e4m3")
    gT = np.abs(n((N, T))).astype(np.float32)
    return {"tab_words": tab_words, "tab_scales": tab_scales, "offs": offs,
            "w1": w1, "wg_words": wg_words, "wg_scales": wg_scales,
            "wo_words": wo_words, "wo_scales": wo_scales, "gT": gT}

def reference(tab_words, tab_scales, offs, w1, wg_words, wg_scales,
              wo_words, wo_scales, gT):
    v = unpack_weight(tab_words, tab_scales, "e4m3")[:, unstriped(offs)]
    a = mxq(f64(w1), 0, "e4m3").T @ v
    b = unpack_weight(wg_words, wg_scales, "e2m1").T @ v
    h = a * (1.0 / (1.0 + np.exp(-b)))
    y = unpack_weight(wo_words, wo_scales, "e4m3").T @ mxq(h, 0, "e4m3")
    g = f64(gT)[:, unstriped(offs)]
    new = np.sqrt(g * g + y * y)
    out = f64(gT).copy()
    out[:, unstriped(offs)] = new
    return out

@@ -1,0 +1,323 @@
+from contextlib import ExitStack
+
+import concourse.mybir as mybir
+from concourse.masks import make_identity
+
+K, T, S, H, N = 1024, 2048, 1024, 1024, 512
+FLOPS = 2 * (2 * K * H * S + H * N * S)
+
+F32 = mybir.dt.float32
+BF16 = mybir.dt.bfloat16
+I32 = mybir.dt.int32
+U32 = mybir.dt.uint32
+U16 = mybir.dt.uint16
+U8 = mybir.dt.uint8
+FP8X4 = mybir.dt.float8_e4m3fn_x4
+FP4X4 = mybir.dt.float4_e2m1fn_x4
+ACT = mybir.ActivationFunctionType
+ALU = mybir.AluOpType
+
+P = 128
+PACK = 4
+KP = P * PACK
+CH = 128
+NCH = S // CH
+HALF = 512
+MOVED = 112
+KIB = 1024
+
+
+def tile_list_sauce_seasoning_kernel(
+    tc, tab_words, tab_scales, offs, w1, wg_words, wg_scales, wo_words, wo_scales, gT, out
+):
+    nc = tc.nc
+    with ExitStack() as ctx:
+        keep = ctx.enter_context(tc.tile_pool(name="keep", bufs=1))
+        shared = ctx.enter_context(tc.tile_pool(name="shared", bufs=1))
+        ring = ctx.enter_context(tc.tile_pool(name="ring", bufs=4))
+        psum = ctx.enter_context(tc.psum_pool(name="psum", bufs=1))
+
+        offsets = keep.tile([P, S // 16], U16, name="offsets")
+        nc.sync.dma_start(offsets[:], offs)
+
+        def half_list(hf):
+            return offsets[:, hf * (HALF // 16) : (hf + 1) * (HALF // 16)]
+
+        def placed(name, kib, shape, dtype):
+            return shared.tile(shape, dtype, name=name, offset=int(kib * KIB), align_bytes=64)
+
+        def load_scales(plane, src):
+            for q in range(4):
+                nc.sync.dma_start(
+                    plane[32 * q : 32 * q + 8, :].bitcast(I32),
+                    src[:, 4 * q : 4 * q + 4, :].bitcast(I32),
+                )
+
+        def second_pass_plane(packed, width, name):
+            plane = keep.tile([P, width], U8, name=name, align_bytes=64)
+            nc.gpsimd.memset(plane[:].bitcast(I32), 0)
+            nc.sync.dma_start(plane[0:MOVED, :].bitcast(I32), packed[4 : 4 + MOVED, :].bitcast(I32))
+            return plane
+
+        w1_raw = {}
+
+        def load_w1(rb, a, kib):
+            raw = placed(f"w1_raw{rb}{a}", kib, [P, PACK, KP], F32)
+            nc.sync.dma_start(
+                raw[:],
+                w1[a * KP : (a + 1) * KP, rb * KP : (rb + 1) * KP].rearrange("(p j) c -> p j c", j=PACK),
+            )
+            w1_raw[rb, a] = raw
+
+        page = {}
+
+        def load_page(nt, kib):
+            rows = placed(f"page{nt}", kib, [P, T], F32)
+            nc.sync.dma_start(rows[:], gT[nt * P : (nt + 1) * P, :])
+            page[nt] = rows
+
+        wg_raw = placed("wg_raw", 0, [P, 2 * 2 * H], U8)
+        nc.sync.dma_start(
+            wg_raw[:].bitcast(I32).rearrange("p (a b) -> p a b", a=2),
+            wg_words.rearrange("a p b -> p a b").bitcast(I32),
+        )
+        tab_sc = placed("tab_sc", 24, [P, T], U8)
+        nc.vector.memset(tab_sc[:].bitcast(I32), 0)
+        load_scales(tab_sc, tab_scales)
+        zeros = placed("zeros", 15.5, [P, H // 4], I32)
+        nc.vector.memset(zeros[:], 0)
+        wg_sc_raw = placed("wg_sc_raw", 90, [P, H], U8)
+        nc.vector.tensor_copy(wg_sc_raw[:].bitcast(I32), zeros[:])
+        tab = []
+        for a, kib in enumerate((8, 16)):
+            words = placed(f"tab{a}", kib, [P, T], I32)
+            nc.sync.dma_start(words[:], tab_words[a].rearrange("p t i -> p (t i)").bitcast(I32))
+            tab.append(words)
+        load_scales(wg_sc_raw, wg_scales)
+
+        ident = keep.tile([P, P], F32, name="ident", align_bytes=64)
+        make_identity(nc, ident[:])
+
+        wg = keep.tile([P, 2 * 2 * H], U8, name="wg", align_bytes=64)
+        nc.vector.tensor_copy(
+            wg[:].bitcast(U16).rearrange("p (g t m) -> p g t m", g=4, t=PACK),
+            wg_raw[:].bitcast(U16).rearrange("p (g m t) -> p g t m", g=4, t=PACK),
+        )
+        load_w1(0, 0, 0)
+        v_sc = keep.tile([P, S], U8, name="v_sc", align_bytes=64)
+        nc.vector.tensor_copy(v_sc[:], tab_sc[:].indirect(offsets[:]))
+        v_planes = [v_sc, second_pass_plane(v_sc, S, "v_sc1")]
+        load_w1(0, 1, 24)
+
+        v = {}
+
+        def pick_words(a, hf, picked):
+            nc.vector.tensor_copy(picked, tab[a][:].bitcast(U32).indirect(half_list(hf)))
+            v[a, hf] = picked
+
+        pick_words(0, 0, keep.tile([P, HALF], U32, name="v_first", align_bytes=64)[:])
+        wg_sc = keep.tile([P, H], U8, name="wg_sc", align_bytes=64)
+        nc.vector.tensor_copy(
+            wg_sc[:].rearrange("p (g t m) -> p g t m", g=2, t=PACK),
+            wg_sc_raw[:].rearrange("p (g m t) -> p g t m", g=2, t=PACK),
+        )
+        wg_planes = [wg_sc, second_pass_plane(wg_sc, H, "wg_sc1")]
+        load_page(0, 90.5)
+        v_rest = placed("v_rest", 84.5, [P, 3 * HALF], U32)
+        pick_words(0, 1, v_rest[:, 0:HALF])
+        wo_sc = placed("wo_sc", 9, [P, N], U8)
+        nc.vector.memset(wo_sc[:].bitcast(I32), 0)
+        load_scales(wo_sc, wo_scales)
+        pick_words(1, 0, v_rest[:, HALF : 2 * HALF])
+        pick_words(1, 1, v_rest[:, 2 * HALF : 3 * HALF])
+
+        def v_codes(a, c):
+            hf, i = divmod(c, 4)
+            return v[a, hf][:, i * CH : (i + 1) * CH].bitcast(FP8X4)
+
+        w1_bf, w1q = {}, {}
+
+        def round_w1(rb, a, kib):
+            grouped = placed(f"w1_bf{rb}{a}", kib, [P, PACK * KP], BF16)
+            nc.scalar.copy(
+                grouped[:].rearrange("p (t m j) -> p m j t", t=PACK, j=PACK),
+                w1_raw[rb, a][:].rearrange("p j (m t) -> p m j t", t=PACK),
+            )
+            w1_bf[rb, a] = grouped
+
+        def quantize_w1(rb, a, codes):
+            scales = keep.tile([P, KP], U8, name=f"w1s{rb}{a}", align_bytes=64)
+            nc.vector.quantize_mx(out=codes[:].bitcast(FP8X4), scales=scales[:], in_=w1_bf[rb, a][:])
+            for t in range(PACK):
+                w1q[rb, a, t] = codes[:, t * P : (t + 1) * P], scales[:, t * P : (t + 1) * P]
+
+        def round_w1_half(rb, a, u, kib, copy):
+            grouped = placed(f"w1_bf{rb}{a}{u}", kib, [P, 2 * KP], BF16)
+            copy(
+                grouped[:].rearrange("p (t m j) -> p m j t", t=2, j=PACK),
+                w1_raw[rb, a][:].rearrange("p j (m t) -> p m j t", t=PACK)[:, :, :, 2 * u : 2 * u + 2],
+            )
+            w1_bf[rb, a, u] = grouped
+
+        def quantize_w1_half(rb, a, u):
+            codes = keep.tile([P, 2 * P], U32, name=f"w1q{rb}{a}{u}", align_bytes=64)
+            scales = keep.tile([P, 2 * P], U8, name=f"w1s{rb}{a}{u}", align_bytes=64)
+            nc.vector.quantize_mx(out=codes[:].bitcast(FP8X4), scales=scales[:], in_=w1_bf[rb, a, u][:])
+            for t in range(2):
+                w1q[rb, a, 2 * u + t] = codes[:, t * P : (t + 1) * P], scales[:, t * P : (t + 1) * P]
+
+        gate, h_bf, hq = {}, {}, {}
+
+        def gates(rb, c, kib):
+            bank = psum.tile([P, PACK, CH], F32, name="b_bank", tag="act", bufs=5)
+            for t in range(PACK):
+                for a in range(2):
+                    col = rb * KP + t * P
+                    nc.tensor.matmul_mx(
+                        out=bank[:, t, :],
+                        lhsT=wg[:, 2 * (a * H + col) : 2 * (a * H + col + P)].bitcast(FP4X4),
+                        lhsT_scale=wg_planes[a][:, col : col + P],
+                        rhs=v_codes(a, c),
+                        rhs_scale=v_planes[a][:, c * CH : (c + 1) * CH],
+                        start=(a == 0),
+                        stop=(a == 1),
+                    )
+            sig = placed(f"gate{rb}{c}", kib, [P, CH, PACK], F32)
+            nc.scalar.activation(sig[:], bank[:].rearrange("p t j -> p j t"), ACT.Sigmoid)
+            gate[rb, c] = sig
+
+        def features(rb, c):
+            bank = psum.tile([P, PACK, CH], F32, name="a_bank", tag="dve", bufs=3)
+            for t in range(PACK):
+                for a in range(2):
+                    wc, ws = w1q[rb, a, t]
+                    nc.tensor.matmul_mx(
+                        out=bank[:, t, :],
+                        lhsT=wc.bitcast(FP8X4),
+                        lhsT_scale=ws,
+                        rhs=v_codes(a, c),
+                        rhs_scale=v_sc[4 * a : P, c * CH : (c + 1) * CH],
+                        start=(a == 0),
+                        stop=(a == 1),
+                    )
+            hb = ring.tile([P, CH * PACK], BF16, name="h_bf", align_bytes=64)
+            nc.vector.tensor_tensor(
+                hb[:].rearrange("p (j t) -> p j t", t=PACK),
+                bank[:].rearrange("p t j -> p j t"),
+                gate[rb, c][:],
+                ALU.mult,
+            )
+            h_bf[rb, c] = hb
+
+        def quantize_h(rb, c):
+            codes = keep.tile([P, CH], U32, name=f"hq{rb}{c}", align_bytes=64)
+            scales = keep.tile([P, CH], U8, name=f"hs{rb}{c}", align_bytes=64)
+            nc.vector.quantize_mx(out=codes[:].bitcast(FP8X4), scales=scales[:], in_=h_bf[rb, c][:])
+            hq[rb, c] = codes, scales
+
+        y_sq, g_pick, g_sq, root = {}, {}, {}, {}
+
+        def seasoning(c):
+            bank = psum.tile([P, N], F32, name="y_bank", tag="act", bufs=5)
+            for rb in range(2):
+                codes, scales = hq[rb, c]
+                nc.tensor.matmul_mx(
+                    out=bank[:],
+                    lhsT=codes[:].bitcast(FP8X4),
+                    lhsT_scale=scales[:],
+                    rhs=wo[:, rb, :].bitcast(FP8X4),
+                    rhs_scale=wo_sc[4 * rb : P, :],
+                    start=(rb == 0),
+                    stop=(rb == 1),
+                )
+            sq = keep.tile([P, N], F32, name=f"y_sq{c}")
+            nc.scalar.activation(sq[:], bank[:], ACT.Square)
+            y_sq[c] = sq
+
+        def pick_intensity(nt, kib):
+            picked = placed(f"g_pick{nt}", kib, [P, S], F32)
+            nc.vector.tensor_copy(picked[:], page[nt][:].indirect(offsets[:]))
+            g_pick[nt] = picked
+
+        def square_intensity(nt, hf):
+            bank = psum.tile([P, 4, P], F32, name="g_bank", tag="act", bufs=5)
+            for i in range(4):
+                c = 4 * hf + i
+                nc.tensor.transpose(bank[:, i, :], g_pick[nt][:, c * CH : (c + 1) * CH], ident[:])
+            sq = keep.tile([P, 4, P], F32, name=f"g_sq{nt}{hf}")
+            nc.scalar.activation(sq[:], bank[:], ACT.Square)
+            g_sq[nt, hf] = sq
+
+        def combine(nt, hf):
+            bank = psum.tile([P, 4, CH], F32, name="sum_bank", tag="act", bufs=5)
+            for i in range(4):
+                c = 4 * hf + i
+                nc.tensor.matmul(
+                    bank[:, i, :], g_sq[nt, hf][:, i, :], ident[:], start=True, stop=False, is_transpose=True
+                )
+                nc.tensor.matmul(
+                    bank[:, i, :], y_sq[c][:, nt * P : (nt + 1) * P], ident[:], start=False, stop=True, is_transpose=True
+                )
+            new = ring.tile([P, HALF], F32, name="root", bufs=3)
+            nc.scalar.activation(new[:], bank[:].rearrange("p i j -> p (i j)"), ACT.Sqrt)
+            root[nt, hf] = new
+
+        def replace(nt, hf):
+            nc.vector.tensor_copy(page[nt][:].indirect(half_list(hf)), root[nt, hf][:])
+
+        load_w1(1, 0, 16)
+        round_w1(0, 0, 44)
+        load_w1(1, 1, 0)
+        quantize_w1(0, 0, keep.tile([P, KP], U32, name="w1q00", align_bytes=64))
+        load_page(1, 44)
+        round_w1_half(0, 1, 0, 52, nc.scalar.copy)
+        round_w1_half(0, 1, 1, 54, nc.vector.tensor_copy)
+        wo = placed("wo", 24, [P, 2, N], I32)
+        nc.sync.dma_start(wo[:], wo_words.rearrange("a p c i -> p a (c i)").bitcast(I32))
+        load_page(2, 28)
+        quantize_w1_half(0, 1, 0)
+        quantize_w1_half(0, 1, 1)
+        pick_intensity(0, 52)
+        for c in range(NCH):
+            gates(0, c, 58 + 2 * c)
+        for c in range(NCH):
+            features(0, c)
+            if c:
+                quantize_h(0, c - 1)
+            if c == 0:
+                round_w1(1, 0, 56)
+                load_page(3, 16)
+            if c == 2:
+                round_w1(1, 1, 60)
+            if c == 4:
+                quantize_w1(1, 0, placed("w1q10", 66, [P, KP], U32))
+        quantize_w1(1, 1, placed("w1q11", 72, [P, KP], U32))
+        quantize_h(0, NCH - 1)
+        pick_intensity(1, 60)
+        for c in range(NCH):
+            gates(1, c, 2 * c if c < 4 else 68 + 2 * c)
+        square_intensity(0, 0)
+        square_intensity(1, 0)
+        for c in range(NCH):
+            features(1, c)
+            if c:
+                quantize_h(1, c - 1)
+                seasoning(c - 1)
+            if c == 4:
+                pick_intensity(2, 74)
+                combine(0, 0)
+                combine(1, 0)
+        quantize_h(1, NCH - 1)
+        seasoning(NCH - 1)
+        pick_intensity(3, 80)
+        replace(0, 0)
+        replace(1, 0)
+        for nt in range(2, 4):
+            square_intensity(nt, 0)
+            combine(nt, 0)
+            replace(nt, 0)
+        for nt in range(4):
+            square_intensity(nt, 1)
+            combine(nt, 1)
+            replace(nt, 1)
+            nc.sync.dma_start(out[nt * P : (nt + 1) * P, :], page[nt][:])

@@ -76,17 +76,31 @@ def tile_list_sauce_seasoning_kernel(
             nc.sync.dma_start(rows[:], gT[nt * P : (nt + 1) * P, :])
             page[nt] = rows
 
-        wg_raw = placed("wg_raw", 0, [P, 2 * 2 * H], U8)
-        nc.sync.dma_start(
-            wg_raw[:].bitcast(I32).rearrange("p (a b) -> p a b", a=2),
-            wg_words.rearrange("a p b -> p a b").bitcast(I32),
-        )
+        wg_raw, wg = {}, {}
+
+        def load_wg(rb, kib):
+            raw = placed(f"wg_raw{rb}", kib, [P, 2 * 2 * KP], U8)
+            nc.sync.dma_start(
+                raw[:].bitcast(I32).rearrange("p (a b) -> p a b", a=2),
+                wg_words[:, :, 2 * rb * KP : 2 * (rb + 1) * KP].rearrange("a p b -> p a b").bitcast(I32),
+            )
+            wg_raw[rb] = raw
+
+        def order_wg(rb, kib):
+            block = placed(f"wg{rb}", kib, [P, 2 * 2 * KP], U8)
+            nc.vector.tensor_copy(
+                block[:].bitcast(U16).rearrange("p (a t m) -> p a t m", a=2, t=PACK),
+                wg_raw[rb][:].bitcast(U16).rearrange("p (a m t) -> p a t m", a=2, t=PACK),
+            )
+            wg[rb] = block
+
+        load_wg(0, 0)
         tab_sc = placed("tab_sc", 24, [P, T], U8)
         nc.vector.memset(tab_sc[:].bitcast(I32), 0)
         load_scales(tab_sc, tab_scales)
         zeros = placed("zeros", 15.5, [P, H // 4], I32)
         nc.vector.memset(zeros[:], 0)
-        wg_sc_raw = placed("wg_sc_raw", 90, [P, H], U8)
+        wg_sc_raw = placed("wg_sc_raw", 139.5, [P, H], U8)
         nc.vector.tensor_copy(wg_sc_raw[:].bitcast(I32), zeros[:])
         tab = []
         for a, kib in enumerate((8, 16)):
@@ -98,16 +112,12 @@ def tile_list_sauce_seasoning_kernel(
         ident = keep.tile([P, P], F32, name="ident", align_bytes=64)
         make_identity(nc, ident[:])
 
-        wg = keep.tile([P, 2 * 2 * H], U8, name="wg", align_bytes=64)
-        nc.vector.tensor_copy(
-            wg[:].bitcast(U16).rearrange("p (g t m) -> p g t m", g=4, t=PACK),
-            wg_raw[:].bitcast(U16).rearrange("p (g m t) -> p g t m", g=4, t=PACK),
-        )
+        order_wg(0, 121)
         load_w1(0, 0, 0)
         v_sc = keep.tile([P, S], U8, name="v_sc", align_bytes=64)
         nc.vector.tensor_copy(v_sc[:], tab_sc[:].indirect(offsets[:]))
         v_planes = [v_sc, second_pass_plane(v_sc, S, "v_sc1")]
-        load_w1(0, 1, 24)
+        load_page(0, 24)
 
         v = {}
 
@@ -122,9 +132,10 @@ def tile_list_sauce_seasoning_kernel(
             wg_sc_raw[:].rearrange("p (g m t) -> p g t m", g=2, t=PACK),
         )
         wg_planes = [wg_sc, second_pass_plane(wg_sc, H, "wg_sc1")]
-        load_page(0, 90.5)
-        v_rest = placed("v_rest", 84.5, [P, 3 * HALF], U32)
+        load_w1(0, 1, 140)
+        v_rest = placed("v_rest", 134, [P, 3 * HALF], U32)
         pick_words(0, 1, v_rest[:, 0:HALF])
+        load_wg(1, 10)
         wo_sc = placed("wo_sc", 9, [P, N], U8)
         nc.vector.memset(wo_sc[:].bitcast(I32), 0)
         load_scales(wo_sc, wo_scales)
@@ -134,6 +145,9 @@ def tile_list_sauce_seasoning_kernel(
         def v_codes(a, c):
             hf, i = divmod(c, 4)
             return v[a, hf][:, i * CH : (i + 1) * CH].bitcast(FP8X4)
+
+        def bank_tile(name, bank, shape):
+            return psum.tile(shape, F32, name=name, offset=bank * 2 * KIB)
 
         w1_bf, w1q = {}, {}
 
@@ -166,16 +180,17 @@ def tile_list_sauce_seasoning_kernel(
             for t in range(2):
                 w1q[rb, a, 2 * u + t] = codes[:, t * P : (t + 1) * P], scales[:, t * P : (t + 1) * P]
 
-        gate, h_bf, hq = {}, {}, {}
+        gate, feature, h_bf, hq = {}, {}, {}, {}
+        group = (8, 4)
 
         def gates(rb, c, kib):
-            bank = psum.tile([P, PACK, CH], F32, name="b_bank", tag="act", bufs=5)
+            bank = bank_tile(f"b{rb}{c}", 3 + (rb * NCH + c) % 5, [P, PACK, CH])
             for t in range(PACK):
                 for a in range(2):
                     col = rb * KP + t * P
                     nc.tensor.matmul_mx(
                         out=bank[:, t, :],
-                        lhsT=wg[:, 2 * (a * H + col) : 2 * (a * H + col + P)].bitcast(FP4X4),
+                        lhsT=wg[rb][:, 2 * (a * KP + t * P) : 2 * (a * KP + (t + 1) * P)].bitcast(FP4X4),
                         lhsT_scale=wg_planes[a][:, col : col + P],
                         rhs=v_codes(a, c),
                         rhs_scale=v_planes[a][:, c * CH : (c + 1) * CH],
@@ -187,7 +202,7 @@ def tile_list_sauce_seasoning_kernel(
             gate[rb, c] = sig
 
         def features(rb, c):
-            bank = psum.tile([P, PACK, CH], F32, name="a_bank", tag="dve", bufs=3)
+            bank = bank_tile(f"a{rb}{c}", (rb * NCH + c) % 3, [P, PACK, CH])
             for t in range(PACK):
                 for a in range(2):
                     wc, ws = w1q[rb, a, t]
@@ -200,31 +215,37 @@ def tile_list_sauce_seasoning_kernel(
                         start=(a == 0),
                         stop=(a == 1),
                     )
-            hb = ring.tile([P, CH * PACK], BF16, name="h_bf", align_bytes=64)
+            feature[rb, c] = bank
+
+        def gate_features(rb, c):
+            bank = feature[rb, c]
+            if c % group[rb] == 0:
+                h_bf[rb, c // group[rb]] = placed(f"h_bf{rb}{c}", 100 + 8 * rb + c, [P, group[rb] * KP], BF16)
+            i = c % group[rb]
             nc.vector.tensor_tensor(
-                hb[:].rearrange("p (j t) -> p j t", t=PACK),
+                h_bf[rb, c // group[rb]][:, i * KP : (i + 1) * KP].rearrange("p (j t) -> p j t", t=PACK),
                 bank[:].rearrange("p t j -> p j t"),
                 gate[rb, c][:],
                 ALU.mult,
             )
-            h_bf[rb, c] = hb
 
-        def quantize_h(rb, c):
-            codes = keep.tile([P, CH], U32, name=f"hq{rb}{c}", align_bytes=64)
-            scales = keep.tile([P, CH], U8, name=f"hs{rb}{c}", align_bytes=64)
-            nc.vector.quantize_mx(out=codes[:].bitcast(FP8X4), scales=scales[:], in_=h_bf[rb, c][:])
-            hq[rb, c] = codes, scales
+        def quantize_h(rb, g, codes):
+            width = group[rb] * CH
+            scales = keep.tile([P, width], U8, name=f"hs{rb}{g}", align_bytes=64)
+            nc.vector.quantize_mx(out=codes[:].bitcast(FP8X4), scales=scales[:], in_=h_bf[rb, g][:])
+            for i in range(group[rb]):
+                hq[rb, g * group[rb] + i] = codes[:, i * CH : (i + 1) * CH], scales[:, i * CH : (i + 1) * CH]
 
         y_sq, g_pick, g_sq, root = {}, {}, {}, {}
 
-        def seasoning(c):
-            bank = psum.tile([P, N], F32, name="y_bank", tag="act", bufs=5)
+        def seasoning(c, b):
+            bank = bank_tile(f"y{c}", b, [P, N])
             for rb in range(2):
                 codes, scales = hq[rb, c]
                 nc.tensor.matmul_mx(
                     out=bank[:],
-                    lhsT=codes[:].bitcast(FP8X4),
-                    lhsT_scale=scales[:],
+                    lhsT=codes.bitcast(FP8X4),
+                    lhsT_scale=scales,
                     rhs=wo[:, rb, :].bitcast(FP8X4),
                     rhs_scale=wo_sc[4 * rb : P, :],
                     start=(rb == 0),
@@ -239,8 +260,8 @@ def tile_list_sauce_seasoning_kernel(
             nc.vector.tensor_copy(picked[:], page[nt][:].indirect(offsets[:]))
             g_pick[nt] = picked
 
-        def square_intensity(nt, hf):
-            bank = psum.tile([P, 4, P], F32, name="g_bank", tag="act", bufs=5)
+        def square_intensity(nt, hf, b):
+            bank = bank_tile(f"g{nt}{hf}", b, [P, 4, P])
             for i in range(4):
                 c = 4 * hf + i
                 nc.tensor.transpose(bank[:, i, :], g_pick[nt][:, c * CH : (c + 1) * CH], ident[:])
@@ -248,15 +269,26 @@ def tile_list_sauce_seasoning_kernel(
             nc.scalar.activation(sq[:], bank[:], ACT.Square)
             g_sq[nt, hf] = sq
 
-        def combine(nt, hf):
-            bank = psum.tile([P, 4, CH], F32, name="sum_bank", tag="act", bufs=5)
+        total = {}
+
+        def open_sum(nt, hf, b):
+            bank = bank_tile(f"sum{nt}{hf}", b, [P, 4, CH])
             for i in range(4):
-                c = 4 * hf + i
                 nc.tensor.matmul(
-                    bank[:, i, :], g_sq[nt, hf][:, i, :], ident[:], start=True, stop=False, is_transpose=True
+                    bank[:, i, :], g_sq[nt, hf][:, i, :], ident[:], start=(i == 0), stop=False, is_transpose=True
                 )
+            total[nt, hf] = bank
+
+        def close_sum(nt, hf):
+            bank = total[nt, hf]
+            for i in range(4):
                 nc.tensor.matmul(
-                    bank[:, i, :], y_sq[c][:, nt * P : (nt + 1) * P], ident[:], start=False, stop=True, is_transpose=True
+                    bank[:, i, :],
+                    y_sq[4 * hf + i][:, nt * P : (nt + 1) * P],
+                    ident[:],
+                    start=False,
+                    stop=(i == 3),
+                    is_transpose=True,
                 )
             new = ring.tile([P, HALF], F32, name="root", bufs=3)
             nc.scalar.activation(new[:], bank[:].rearrange("p i j -> p (i j)"), ACT.Sqrt)
@@ -266,58 +298,65 @@ def tile_list_sauce_seasoning_kernel(
             nc.vector.tensor_copy(page[nt][:].indirect(half_list(hf)), root[nt, hf][:])
 
         load_w1(1, 0, 16)
+        pick_intensity(0, 74)
         round_w1(0, 0, 44)
         load_w1(1, 1, 0)
         quantize_w1(0, 0, keep.tile([P, KP], U32, name="w1q00", align_bytes=64))
         load_page(1, 44)
         round_w1_half(0, 1, 0, 52, nc.scalar.copy)
         round_w1_half(0, 1, 1, 54, nc.vector.tensor_copy)
-        wo = placed("wo", 24, [P, 2, N], I32)
+        wo = placed("wo", 140, [P, 2, N], I32)
         nc.sync.dma_start(wo[:], wo_words.rearrange("a p c i -> p a (c i)").bitcast(I32))
-        load_page(2, 28)
+        load_page(2, 144)
         quantize_w1_half(0, 1, 0)
         quantize_w1_half(0, 1, 1)
-        pick_intensity(0, 52)
         for c in range(NCH):
             gates(0, c, 58 + 2 * c)
+        round_w1(1, 0, 118)
+        load_page(3, 16)
+        round_w1(1, 1, 122)
         for c in range(NCH):
             features(0, c)
-            if c:
-                quantize_h(0, c - 1)
-            if c == 0:
-                round_w1(1, 0, 56)
-                load_page(3, 16)
-            if c == 2:
-                round_w1(1, 1, 60)
-            if c == 4:
-                quantize_w1(1, 0, placed("w1q10", 66, [P, KP], U32))
-        quantize_w1(1, 1, placed("w1q11", 72, [P, KP], U32))
-        quantize_h(0, NCH - 1)
-        pick_intensity(1, 60)
-        for c in range(NCH):
-            gates(1, c, 2 * c if c < 4 else 68 + 2 * c)
-        square_intensity(0, 0)
-        square_intensity(1, 0)
-        for c in range(NCH):
+            gate_features(0, c)
+        order_wg(1, 68)
+        quantize_w1(1, 0, placed("w1q10", 72, [P, KP], U32))
+        pick_intensity(1, 116)
+        quantize_w1(1, 1, placed("w1q11", 120, [P, KP], U32))
+        quantize_h(0, 0, placed("hq0", 122, [P, S], U32))
+        for c in range(5):
+            gates(1, c, 2 * c if c < 4 else 118 + 2 * c)
+        for c in range(5):
             features(1, c)
-            if c:
-                quantize_h(1, c - 1)
-                seasoning(c - 1)
-            if c == 4:
-                pick_intensity(2, 74)
-                combine(0, 0)
-                combine(1, 0)
-        quantize_h(1, NCH - 1)
-        seasoning(NCH - 1)
-        pick_intensity(3, 80)
+            gate_features(1, c)
+        for c in range(5, NCH):
+            gates(1, c, 118 + 2 * c)
+            features(1, c)
+        square_intensity(0, 0, 4)
+        square_intensity(1, 0, 5)
+        open_sum(0, 0, 6)
+        open_sum(1, 0, 7)
+        quantize_h(1, 0, keep.tile([P, HALF], U32, name="hq10", align_bytes=64))
+        pick_intensity(2, 108)
+        for c, b in enumerate((3, 4, 5, 3)):
+            seasoning(c, b)
+        close_sum(0, 0)
+        close_sum(1, 0)
+        for c in range(5, NCH):
+            gate_features(1, c)
+        quantize_h(1, 1, keep.tile([P, HALF], U32, name="hq11", align_bytes=64))
+        pick_intensity(3, 112)
         replace(0, 0)
         replace(1, 0)
-        for nt in range(2, 4):
-            square_intensity(nt, 0)
-            combine(nt, 0)
+        for nt, (b_square, b_sum) in ((2, (4, 5)), (3, (6, 7))):
+            square_intensity(nt, 0, b_square)
+            open_sum(nt, 0, b_sum)
+            close_sum(nt, 0)
             replace(nt, 0)
-        for nt in range(4):
-            square_intensity(nt, 1)
-            combine(nt, 1)
+        for c, b in zip(range(4, NCH), (1, 2, 0, 1)):
+            seasoning(c, b)
+        for nt, (b_square, b_sum) in enumerate(((4, 3), (2, 5), (0, 6), (1, 7))):
+            square_intensity(nt, 1, b_square)
+            open_sum(nt, 1, b_sum)
+            close_sum(nt, 1)
             replace(nt, 1)
             nc.sync.dma_start(out[nt * P : (nt + 1) * P, :], page[nt][:])

@@ -25,6 +25,8 @@ NCH = S // CH
 HALF = 512
 MOVED = 112
 KIB = 1024
+GATE_BANKS = ((0, 1, 2, 3, 4, 5, 6, 7), (3, 4, 2, 5, 6, 7, 0, 1))
+FEATURE_BANKS = ((0, 1, 2, 5, 6, 7, 0, 1), (3, 4, 2, 5, 6, 7, 0, 1))
 
 
 def tile_list_sauce_seasoning_kernel(
@@ -95,19 +97,23 @@ def tile_list_sauce_seasoning_kernel(
             wg[rb] = block
 
         load_wg(0, 0)
-        tab_sc = placed("tab_sc", 24, [P, T], U8)
+        tab_sc = placed("tab_sc", 32, [P, T], U8)
         nc.vector.memset(tab_sc[:].bitcast(I32), 0)
         load_scales(tab_sc, tab_scales)
-        zeros = placed("zeros", 15.5, [P, H // 4], I32)
+        zeros = placed("zeros", 17.5, [P, H // 4], I32)
         nc.vector.memset(zeros[:], 0)
-        wg_sc_raw = placed("wg_sc_raw", 139.5, [P, H], U8)
+        wg_sc_raw = placed("wg_sc_raw", 142, [P, H], U8)
         nc.vector.tensor_copy(wg_sc_raw[:].bitcast(I32), zeros[:])
-        tab = []
-        for a, kib in enumerate((8, 16)):
+        tab = {}
+
+        def load_words(a, kib):
             words = placed(f"tab{a}", kib, [P, T], I32)
             nc.sync.dma_start(words[:], tab_words[a].rearrange("p t i -> p (t i)").bitcast(I32))
-            tab.append(words)
+            tab[a] = words
+
+        load_words(0, 10)
         load_scales(wg_sc_raw, wg_scales)
+        load_words(1, 18)
 
         ident = keep.tile([P, P], F32, name="ident", align_bytes=64)
         make_identity(nc, ident[:])
@@ -117,34 +123,35 @@ def tile_list_sauce_seasoning_kernel(
         v_sc = keep.tile([P, S], U8, name="v_sc", align_bytes=64)
         nc.vector.tensor_copy(v_sc[:], tab_sc[:].indirect(offsets[:]))
         v_planes = [v_sc, second_pass_plane(v_sc, S, "v_sc1")]
-        load_page(0, 24)
-
-        v = {}
-
-        def pick_words(a, hf, picked):
-            nc.vector.tensor_copy(picked, tab[a][:].bitcast(U32).indirect(half_list(hf)))
-            v[a, hf] = picked
-
-        pick_words(0, 0, keep.tile([P, HALF], U32, name="v_first", align_bytes=64)[:])
+        load_wg(1, 32)
         wg_sc = keep.tile([P, H], U8, name="wg_sc", align_bytes=64)
         nc.vector.tensor_copy(
             wg_sc[:].rearrange("p (g t m) -> p g t m", g=2, t=PACK),
             wg_sc_raw[:].rearrange("p (g m t) -> p g t m", g=2, t=PACK),
         )
         wg_planes = [wg_sc, second_pass_plane(wg_sc, H, "wg_sc1")]
-        load_w1(0, 1, 140)
-        v_rest = placed("v_rest", 134, [P, 3 * HALF], U32)
-        pick_words(0, 1, v_rest[:, 0:HALF])
-        load_wg(1, 10)
-        wo_sc = placed("wo_sc", 9, [P, N], U8)
+        load_page(0, 142.5)
+
+        v = placed("v", 134.5, [P, 4 * HALF], U32)
+
+        def v_columns(a, first, count):
+            start = (first // HALF * 2 + a) * HALF + first % HALF
+            return v[:, start : start + count]
+
+        for hf in range(2):
+            for a in range(2):
+                nc.vector.tensor_copy(
+                    v_columns(a, hf * HALF, HALF), tab[a][:].bitcast(U32).indirect(half_list(hf))
+                )
+        load_w1(0, 1, 10)
+        load_w1(1, 0, 23)
+        order_wg(1, 21)
+        wo_sc = placed("wo_sc", 20, [P, N], U8)
         nc.vector.memset(wo_sc[:].bitcast(I32), 0)
         load_scales(wo_sc, wo_scales)
-        pick_words(1, 0, v_rest[:, HALF : 2 * HALF])
-        pick_words(1, 1, v_rest[:, 2 * HALF : 3 * HALF])
 
         def v_codes(a, c):
-            hf, i = divmod(c, 4)
-            return v[a, hf][:, i * CH : (i + 1) * CH].bitcast(FP8X4)
+            return v_columns(a, c * CH, CH).bitcast(FP8X4)
 
         def bank_tile(name, bank, shape):
             return psum.tile(shape, F32, name=name, offset=bank * 2 * KIB)
@@ -154,8 +161,8 @@ def tile_list_sauce_seasoning_kernel(
         def round_w1(rb, a, kib):
             grouped = placed(f"w1_bf{rb}{a}", kib, [P, PACK * KP], BF16)
             nc.scalar.copy(
-                grouped[:].rearrange("p (t m j) -> p m j t", t=PACK, j=PACK),
-                w1_raw[rb, a][:].rearrange("p j (m t) -> p m j t", t=PACK),
+                grouped[:].rearrange("p (t m e j) -> p m j e t", t=PACK, e=2, j=PACK),
+                w1_raw[rb, a][:].rearrange("p j (m e t) -> p m j e t", e=2, t=PACK),
             )
             w1_bf[rb, a] = grouped
 
@@ -168,8 +175,8 @@ def tile_list_sauce_seasoning_kernel(
         def round_w1_half(rb, a, u, kib, copy):
             grouped = placed(f"w1_bf{rb}{a}{u}", kib, [P, 2 * KP], BF16)
             copy(
-                grouped[:].rearrange("p (t m j) -> p m j t", t=2, j=PACK),
-                w1_raw[rb, a][:].rearrange("p j (m t) -> p m j t", t=PACK)[:, :, :, 2 * u : 2 * u + 2],
+                grouped[:].rearrange("p (t m e j) -> p m j e t", t=2, e=2, j=PACK),
+                w1_raw[rb, a][:].rearrange("p j (m e t) -> p m j e t", e=2, t=PACK)[:, :, :, :, 2 * u : 2 * u + 2],
             )
             w1_bf[rb, a, u] = grouped
 
@@ -184,7 +191,7 @@ def tile_list_sauce_seasoning_kernel(
         group = (8, 4)
 
         def gates(rb, c, kib):
-            bank = bank_tile(f"b{rb}{c}", 3 + (rb * NCH + c) % 5, [P, PACK, CH])
+            bank = bank_tile(f"b{rb}{c}", GATE_BANKS[rb][c], [P, PACK, CH])
             for t in range(PACK):
                 for a in range(2):
                     col = rb * KP + t * P
@@ -202,7 +209,7 @@ def tile_list_sauce_seasoning_kernel(
             gate[rb, c] = sig
 
         def features(rb, c):
-            bank = bank_tile(f"a{rb}{c}", (rb * NCH + c) % 3, [P, PACK, CH])
+            bank = bank_tile(f"a{rb}{c}", FEATURE_BANKS[rb][c], [P, PACK, CH])
             for t in range(PACK):
                 for a in range(2):
                     wc, ws = w1q[rb, a, t]
@@ -297,49 +304,45 @@ def tile_list_sauce_seasoning_kernel(
         def replace(nt, hf):
             nc.vector.tensor_copy(page[nt][:].indirect(half_list(hf)), root[nt, hf][:])
 
-        load_w1(1, 0, 16)
         pick_intensity(0, 74)
         round_w1(0, 0, 44)
         load_w1(1, 1, 0)
         quantize_w1(0, 0, keep.tile([P, KP], U32, name="w1q00", align_bytes=64))
         load_page(1, 44)
-        round_w1_half(0, 1, 0, 52, nc.scalar.copy)
+        round_w1_half(0, 1, 0, 52, nc.vector.tensor_copy)
         round_w1_half(0, 1, 1, 54, nc.vector.tensor_copy)
-        wo = placed("wo", 140, [P, 2, N], I32)
+        wo = placed("wo", 8, [P, 2, N], I32)
         nc.sync.dma_start(wo[:], wo_words.rearrange("a p c i -> p a (c i)").bitcast(I32))
-        load_page(2, 144)
+        load_page(2, 12)
         quantize_w1_half(0, 1, 0)
         quantize_w1_half(0, 1, 1)
         for c in range(NCH):
             gates(0, c, 58 + 2 * c)
         round_w1(1, 0, 118)
-        load_page(3, 16)
+        load_page(3, 23)
         round_w1(1, 1, 122)
         for c in range(NCH):
             features(0, c)
             gate_features(0, c)
-        order_wg(1, 68)
         quantize_w1(1, 0, placed("w1q10", 72, [P, KP], U32))
         pick_intensity(1, 116)
         quantize_w1(1, 1, placed("w1q11", 120, [P, KP], U32))
         quantize_h(0, 0, placed("hq0", 122, [P, S], U32))
-        for c in range(5):
+        for c in range(NCH):
             gates(1, c, 2 * c if c < 4 else 118 + 2 * c)
+        for c in range(NCH):
+            features(1, c)
         for c in range(5):
-            features(1, c)
             gate_features(1, c)
-        for c in range(5, NCH):
-            gates(1, c, 118 + 2 * c)
-            features(1, c)
-        square_intensity(0, 0, 4)
-        square_intensity(1, 0, 5)
-        open_sum(0, 0, 6)
-        open_sum(1, 0, 7)
+        square_intensity(0, 0, 3)
+        open_sum(0, 0, 4)
         quantize_h(1, 0, keep.tile([P, HALF], U32, name="hq10", align_bytes=64))
         pick_intensity(2, 108)
-        for c, b in enumerate((3, 4, 5, 3)):
+        for c, b in enumerate((3, 2, 5, 6)):
             seasoning(c, b)
         close_sum(0, 0)
+        square_intensity(1, 0, 3)
+        open_sum(1, 0, 2)
         close_sum(1, 0)
         for c in range(5, NCH):
             gate_features(1, c)
@@ -347,14 +350,14 @@ def tile_list_sauce_seasoning_kernel(
         pick_intensity(3, 112)
         replace(0, 0)
         replace(1, 0)
-        for nt, (b_square, b_sum) in ((2, (4, 5)), (3, (6, 7))):
+        for nt, (b_square, b_sum) in ((2, (5, 6)), (3, (4, 2))):
             square_intensity(nt, 0, b_square)
             open_sum(nt, 0, b_sum)
             close_sum(nt, 0)
             replace(nt, 0)
-        for c, b in zip(range(4, NCH), (1, 2, 0, 1)):
+        for c, b in zip(range(4, NCH), (7, 0, 1, 7)):
             seasoning(c, b)
-        for nt, (b_square, b_sum) in enumerate(((4, 3), (2, 5), (0, 6), (1, 7))):
+        for nt, (b_square, b_sum) in enumerate(((3, 5), (0, 6), (1, 4), (7, 2))):
             square_intensity(nt, 1, b_square)
             open_sum(nt, 1, b_sum)
             close_sum(nt, 1)

@@ -23,10 +23,7 @@ KP = P * PACK
 CH = 128
 NCH = S // CH
 HALF = 512
-MOVED = 112
 KIB = 1024
-GATE_BANKS = ((0, 1, 2, 3, 4, 5, 6, 7), (3, 4, 2, 5, 6, 7, 0, 1))
-FEATURE_BANKS = ((0, 1, 2, 5, 6, 7, 0, 1), (3, 4, 2, 5, 6, 7, 0, 1))
 
 
 def tile_list_sauce_seasoning_kernel(
@@ -36,8 +33,16 @@ def tile_list_sauce_seasoning_kernel(
     with ExitStack() as ctx:
         keep = ctx.enter_context(tc.tile_pool(name="keep", bufs=1))
         shared = ctx.enter_context(tc.tile_pool(name="shared", bufs=1))
-        ring = ctx.enter_context(tc.tile_pool(name="ring", bufs=4))
         psum = ctx.enter_context(tc.psum_pool(name="psum", bufs=1))
+
+        def kept(name, shape, dtype):
+            return keep.tile(shape, dtype, name=name, align_bytes=64)
+
+        def placed(name, kib, shape, dtype):
+            return shared.tile(shape, dtype, name=name, offset=int(kib * KIB), align_bytes=64)
+
+        def bank_tile(name, bank, shape):
+            return psum.tile(shape, F32, name=name, offset=bank * 2 * KIB)
 
         offsets = keep.tile([P, S // 16], U16, name="offsets")
         nc.sync.dma_start(offsets[:], offs)
@@ -45,23 +50,19 @@ def tile_list_sauce_seasoning_kernel(
         def half_list(hf):
             return offsets[:, hf * (HALF // 16) : (hf + 1) * (HALF // 16)]
 
-        def placed(name, kib, shape, dtype):
-            return shared.tile(shape, dtype, name=name, offset=int(kib * KIB), align_bytes=64)
-
-        def load_scales(plane, src):
+        def load_packed_scales(plane, src):
             for q in range(4):
                 nc.sync.dma_start(
                     plane[32 * q : 32 * q + 8, :].bitcast(I32),
                     src[:, 4 * q : 4 * q + 4, :].bitcast(I32),
                 )
 
-        def second_pass_plane(packed, width, name):
-            plane = keep.tile([P, width], U8, name=name, align_bytes=64)
-            nc.gpsimd.memset(plane[:].bitcast(I32), 0)
-            nc.sync.dma_start(plane[0:MOVED, :].bitcast(I32), packed[4 : 4 + MOVED, :].bitcast(I32))
-            return plane
+        tab, w1_raw, page = {}, {}, {}
 
-        w1_raw = {}
+        def load_words(a, kib):
+            words = placed(f"tab{a}", kib, [P, T], I32)
+            nc.sync.dma_start(words[:], tab_words[a].rearrange("p t i -> p (t i)").bitcast(I32))
+            tab[a] = words
 
         def load_w1(rb, a, kib):
             raw = placed(f"w1_raw{rb}{a}", kib, [P, PACK, KP], F32)
@@ -71,134 +72,131 @@ def tile_list_sauce_seasoning_kernel(
             )
             w1_raw[rb, a] = raw
 
-        page = {}
-
         def load_page(nt, kib):
             rows = placed(f"page{nt}", kib, [P, T], F32)
             nc.sync.dma_start(rows[:], gT[nt * P : (nt + 1) * P, :])
             page[nt] = rows
 
-        wg_raw, wg = {}, {}
-
-        def load_wg(rb, kib):
-            raw = placed(f"wg_raw{rb}", kib, [P, 2 * 2 * KP], U8)
+        wg_raw = placed("wg_raw", 37, [P, 2, 2 * H], U8)
+        nc.sync.dma_start(wg_raw[:].bitcast(I32), wg_words.rearrange("a p b -> p a b").bitcast(I32))
+        tab_sc = placed("tab_sc", 0, [P, T], U8)
+        nc.vector.memset(tab_sc[:].bitcast(I32), 0)
+        load_packed_scales(tab_sc, tab_scales)
+        zero_a = placed("zero_a", 8, [P, 32], I32)
+        nc.gpsimd.memset(zero_a[:], 0)
+        zero_b = placed("zero_b", 24 - 1 / 16, [P, 32], I32)
+        nc.gpsimd.memset(zero_b[:], 0)
+        v_sc1 = kept("v_sc1", [P, S], U8)
+        nc.vector.tensor_copy(
+            v_sc1[:].bitcast(I32).rearrange("p (r w) -> p r w", w=32),
+            zero_a[:].unsqueeze(1).to_broadcast([P, 8, 32]),
+        )
+        wg_sc_raw = placed("wg_sc_raw", 41, [P, 2, H], U8)
+        nc.vector.tensor_copy(
+            wg_sc_raw[:].bitcast(I32).rearrange("p a (r w) -> p (a r) w", w=32),
+            zero_b[:].unsqueeze(1).to_broadcast([P, 16, 32]),
+        )
+        load_words(0, 8)
+        for q in range(4):
             nc.sync.dma_start(
-                raw[:].bitcast(I32).rearrange("p (a b) -> p a b", a=2),
-                wg_words[:, :, 2 * rb * KP : 2 * (rb + 1) * KP].rearrange("a p b -> p a b").bitcast(I32),
+                wg_sc_raw[32 * q : 32 * q + 4, :, :].bitcast(I32),
+                wg_scales[:, 4 * q : 4 * q + 4, :].rearrange("a r h -> r a h").bitcast(I32),
             )
-            wg_raw[rb] = raw
+        load_words(1, 24)
+        load_w1(0, 0, 16)
 
-        def order_wg(rb, kib):
-            block = placed(f"wg{rb}", kib, [P, 2 * 2 * KP], U8)
+        wg = {}
+        for rb in range(2):
+            block = kept(f"wg{rb}", [P, 2 * 2 * KP], U8)
             nc.vector.tensor_copy(
                 block[:].bitcast(U16).rearrange("p (a t m) -> p a t m", a=2, t=PACK),
-                wg_raw[rb][:].bitcast(U16).rearrange("p (a m t) -> p a t m", a=2, t=PACK),
+                wg_raw[:].bitcast(U16)[:, :, rb * KP : (rb + 1) * KP].rearrange("p a (m t) -> p a t m", t=PACK),
             )
             wg[rb] = block
-
-        load_wg(0, 0)
-        tab_sc = placed("tab_sc", 32, [P, T], U8)
-        nc.vector.memset(tab_sc[:].bitcast(I32), 0)
-        load_scales(tab_sc, tab_scales)
-        zeros = placed("zeros", 17.5, [P, H // 4], I32)
-        nc.vector.memset(zeros[:], 0)
-        wg_sc_raw = placed("wg_sc_raw", 142, [P, H], U8)
-        nc.vector.tensor_copy(wg_sc_raw[:].bitcast(I32), zeros[:])
-        tab = {}
-
-        def load_words(a, kib):
-            words = placed(f"tab{a}", kib, [P, T], I32)
-            nc.sync.dma_start(words[:], tab_words[a].rearrange("p t i -> p (t i)").bitcast(I32))
-            tab[a] = words
-
-        load_words(0, 10)
-        load_scales(wg_sc_raw, wg_scales)
-        load_words(1, 18)
-
-        ident = keep.tile([P, P], F32, name="ident", align_bytes=64)
-        make_identity(nc, ident[:])
-
-        order_wg(0, 121)
-        load_w1(0, 0, 0)
-        v_sc = keep.tile([P, S], U8, name="v_sc", align_bytes=64)
+        v_sc = kept("v_sc", [P, S], U8)
         nc.vector.tensor_copy(v_sc[:], tab_sc[:].indirect(offsets[:]))
-        v_planes = [v_sc, second_pass_plane(v_sc, S, "v_sc1")]
-        load_wg(1, 32)
-        wg_sc = keep.tile([P, H], U8, name="wg_sc", align_bytes=64)
-        nc.vector.tensor_copy(
-            wg_sc[:].rearrange("p (g t m) -> p g t m", g=2, t=PACK),
-            wg_sc_raw[:].rearrange("p (g m t) -> p g t m", g=2, t=PACK),
-        )
-        wg_planes = [wg_sc, second_pass_plane(wg_sc, H, "wg_sc1")]
-        load_page(0, 142.5)
+        for q in range(4):
+            nc.sync.dma_start(
+                v_sc1[32 * q : 32 * q + 4, :].bitcast(I32), v_sc[32 * q + 4 : 32 * q + 8, :].bitcast(I32)
+            )
+        v_planes = [v_sc, v_sc1]
+        ident = kept("ident", [P, P], F32)
+        make_identity(nc, ident[:])
+        table_warm = kept("table_warm", [P, 1], F32)
+        nc.scalar.activation(table_warm[:], ident[:, 0:1], ACT.Sigmoid)
+        load_w1(0, 1, 0)
 
-        v = placed("v", 134.5, [P, 4 * HALF], U32)
+        v = {}
 
-        def v_columns(a, first, count):
-            start = (first // HALF * 2 + a) * HALF + first % HALF
-            return v[:, start : start + count]
-
-        for hf in range(2):
-            for a in range(2):
-                nc.vector.tensor_copy(
-                    v_columns(a, hf * HALF, HALF), tab[a][:].bitcast(U32).indirect(half_list(hf))
-                )
-        load_w1(0, 1, 10)
-        load_w1(1, 0, 23)
-        order_wg(1, 21)
-        wo_sc = placed("wo_sc", 20, [P, N], U8)
-        nc.vector.memset(wo_sc[:].bitcast(I32), 0)
-        load_scales(wo_sc, wo_scales)
+        def gather_words(a, hf):
+            words = kept(f"v{a}{hf}", [P, HALF], U32)
+            nc.vector.tensor_copy(words[:], tab[a][:].bitcast(U32).indirect(half_list(hf)))
+            v[a, hf] = words
 
         def v_codes(a, c):
-            return v_columns(a, c * CH, CH).bitcast(FP8X4)
+            return v[a, c // 4][:, c % 4 * CH : (c % 4 + 1) * CH].bitcast(FP8X4)
 
-        def bank_tile(name, bank, shape):
-            return psum.tile(shape, F32, name=name, offset=bank * 2 * KIB)
+        gather_words(0, 0)
+        gather_words(0, 1)
+        load_page(0, 8)
+        wg_sc = kept("wg_sc", [P, 2 * H], U8)
+        nc.vector.tensor_copy(
+            wg_sc[:].rearrange("p (g t m) -> p g t m", g=4, t=PACK),
+            wg_sc_raw[:].rearrange("p a (g m t) -> p (a g) t m", g=2, t=PACK),
+        )
+        load_w1(1, 0, 37)
+        gather_words(1, 0)
+        gather_words(1, 1)
+        load_w1(1, 1, 28.5)
+        wo = placed("wo", 24, [P, 2, N], I32)
+        nc.sync.dma_start(wo[:], wo_words.rearrange("a p c i -> p a (c i)").bitcast(I32))
+        wo_sc = placed("wo_sc", 28, [P, N], U8)
+        nc.gpsimd.memset(wo_sc[:].bitcast(I32), 0)
+        load_packed_scales(wo_sc, wo_scales)
 
         w1_bf, w1q = {}, {}
 
-        def round_w1(rb, a, kib):
-            grouped = placed(f"w1_bf{rb}{a}", kib, [P, PACK * KP], BF16)
-            nc.scalar.copy(
+        def round_w1(rb, a, copy):
+            grouped = placed(f"w1_bf{rb}{a}", (150, 160, 166, 174)[2 * rb + a], [P, PACK * KP], BF16)
+            copy(
                 grouped[:].rearrange("p (t m e j) -> p m j e t", t=PACK, e=2, j=PACK),
                 w1_raw[rb, a][:].rearrange("p j (m e t) -> p m j e t", e=2, t=PACK),
             )
-            w1_bf[rb, a] = grouped
+            w1_bf[rb, a] = grouped[:]
 
-        def quantize_w1(rb, a, codes):
-            scales = keep.tile([P, KP], U8, name=f"w1s{rb}{a}", align_bytes=64)
-            nc.vector.quantize_mx(out=codes[:].bitcast(FP8X4), scales=scales[:], in_=w1_bf[rb, a][:])
-            for t in range(PACK):
-                w1q[rb, a, t] = codes[:, t * P : (t + 1) * P], scales[:, t * P : (t + 1) * P]
+        def round_w1_aside(rb, a):
+            grouped = placed(f"w1_bf{rb}{a}", 166, [P, PACK, P, PACK], BF16)
+            for u in range(2):
+                nc.gpsimd.tensor_scalar(
+                    grouped[:, 2 * u : 2 * u + 2, :, :],
+                    w1_raw[rb, a][:].rearrange("p j (m t) -> p t m j", t=PACK)[:, 2 * u : 2 * u + 2, :, :],
+                    1.0,
+                    0.0,
+                    ALU.mult,
+                    ALU.add,
+                )
+            w1_bf[rb, a] = grouped[:].rearrange("p t m j -> p (t m j)")
 
-        def round_w1_half(rb, a, u, kib, copy):
-            grouped = placed(f"w1_bf{rb}{a}{u}", kib, [P, 2 * KP], BF16)
-            copy(
-                grouped[:].rearrange("p (t m e j) -> p m j e t", t=2, e=2, j=PACK),
-                w1_raw[rb, a][:].rearrange("p j (m e t) -> p m j e t", e=2, t=PACK)[:, :, :, :, 2 * u : 2 * u + 2],
-            )
-            w1_bf[rb, a, u] = grouped
+        def quantize(name, src, width):
+            codes = kept(f"{name}_codes", [P, width], U32)
+            scales = kept(f"{name}_scales", [P, width], U8)
+            nc.vector.quantize_mx(out=codes[:].bitcast(FP8X4), scales=scales[:], in_=src)
+            return [(codes[:, i : i + P], scales[:, i : i + P]) for i in range(0, width, P)]
 
-        def quantize_w1_half(rb, a, u):
-            codes = keep.tile([P, 2 * P], U32, name=f"w1q{rb}{a}{u}", align_bytes=64)
-            scales = keep.tile([P, 2 * P], U8, name=f"w1s{rb}{a}{u}", align_bytes=64)
-            nc.vector.quantize_mx(out=codes[:].bitcast(FP8X4), scales=scales[:], in_=w1_bf[rb, a, u][:])
-            for t in range(2):
-                w1q[rb, a, 2 * u + t] = codes[:, t * P : (t + 1) * P], scales[:, t * P : (t + 1) * P]
+        def quantize_w1(rb, a):
+            w1q[rb, a] = quantize(f"w1q{rb}{a}", w1_bf[rb, a], KP)
 
         gate, feature, h_bf, hq = {}, {}, {}, {}
-        group = (8, 4)
 
-        def gates(rb, c, kib):
-            bank = bank_tile(f"b{rb}{c}", GATE_BANKS[rb][c], [P, PACK, CH])
+        def gates(rb, c, b, kib):
+            bank = bank_tile(f"b{rb}{c}", b, [P, PACK, CH])
             for t in range(PACK):
                 for a in range(2):
-                    col = rb * KP + t * P
+                    col = a * H + rb * KP + t * P
                     nc.tensor.matmul_mx(
                         out=bank[:, t, :],
                         lhsT=wg[rb][:, 2 * (a * KP + t * P) : 2 * (a * KP + (t + 1) * P)].bitcast(FP4X4),
-                        lhsT_scale=wg_planes[a][:, col : col + P],
+                        lhsT_scale=wg_sc[:, col : col + P],
                         rhs=v_codes(a, c),
                         rhs_scale=v_planes[a][:, c * CH : (c + 1) * CH],
                         start=(a == 0),
@@ -208,11 +206,11 @@ def tile_list_sauce_seasoning_kernel(
             nc.scalar.activation(sig[:], bank[:].rearrange("p t j -> p j t"), ACT.Sigmoid)
             gate[rb, c] = sig
 
-        def features(rb, c):
-            bank = bank_tile(f"a{rb}{c}", FEATURE_BANKS[rb][c], [P, PACK, CH])
+        def features(rb, c, b):
+            bank = bank_tile(f"a{rb}{c}", b, [P, PACK, CH])
             for t in range(PACK):
                 for a in range(2):
-                    wc, ws = w1q[rb, a, t]
+                    wc, ws = w1q[rb, a][t]
                     nc.tensor.matmul_mx(
                         out=bank[:, t, :],
                         lhsT=wc.bitcast(FP8X4),
@@ -224,26 +222,37 @@ def tile_list_sauce_seasoning_kernel(
                     )
             feature[rb, c] = bank
 
+        def open_h(parts, kib):
+            rows = placed(f"h_bf{parts[0][0]}{parts[0][1]}", kib, [P, len(parts) * KP], BF16)
+            for i, part in enumerate(parts):
+                h_bf[part] = rows[:, i * KP : (i + 1) * KP]
+            return parts, rows
+
         def gate_features(rb, c):
-            bank = feature[rb, c]
-            if c % group[rb] == 0:
-                h_bf[rb, c // group[rb]] = placed(f"h_bf{rb}{c}", 100 + 8 * rb + c, [P, group[rb] * KP], BF16)
-            i = c % group[rb]
             nc.vector.tensor_tensor(
-                h_bf[rb, c // group[rb]][:, i * KP : (i + 1) * KP].rearrange("p (j t) -> p j t", t=PACK),
-                bank[:].rearrange("p t j -> p j t"),
+                h_bf[rb, c].rearrange("p (j t) -> p j t", t=PACK),
+                feature[rb, c][:].rearrange("p t j -> p j t"),
                 gate[rb, c][:],
                 ALU.mult,
             )
 
-        def quantize_h(rb, g, codes):
-            width = group[rb] * CH
-            scales = keep.tile([P, width], U8, name=f"hs{rb}{g}", align_bytes=64)
-            nc.vector.quantize_mx(out=codes[:].bitcast(FP8X4), scales=scales[:], in_=h_bf[rb, g][:])
-            for i in range(group[rb]):
-                hq[rb, g * group[rb] + i] = codes[:, i * CH : (i + 1) * CH], scales[:, i * CH : (i + 1) * CH]
+        def gate_features_aside(rb, c, kib):
+            plain = placed(f"a_plain{rb}{c}", kib, [P, CH, PACK], F32)
+            nc.scalar.copy(plain[:], feature[rb, c][:].rearrange("p t j -> p j t"))
+            nc.gpsimd.tensor_tensor(
+                h_bf[rb, c],
+                plain[:].rearrange("p j t -> p (j t)"),
+                gate[rb, c][:].rearrange("p j t -> p (j t)"),
+                ALU.mult,
+            )
 
-        y_sq, g_pick, g_sq, root = {}, {}, {}, {}
+        def quantize_h(group):
+            parts, rows = group
+            made = quantize(f"hq{parts[0][0]}{parts[0][1]}", rows[:], len(parts) * CH)
+            for part, operand in zip(parts, made):
+                hq[part] = operand
+
+        y_sq, g_pick, g_sq = {}, {}, {}
 
         def seasoning(c, b):
             bank = bank_tile(f"y{c}", b, [P, N])
@@ -258,7 +267,7 @@ def tile_list_sauce_seasoning_kernel(
                     start=(rb == 0),
                     stop=(rb == 1),
                 )
-            sq = keep.tile([P, N], F32, name=f"y_sq{c}")
+            sq = placed(f"y_sq{c}", 102 + 2 * c, [P, N], F32)
             nc.scalar.activation(sq[:], bank[:], ACT.Square)
             y_sq[c] = sq
 
@@ -272,22 +281,16 @@ def tile_list_sauce_seasoning_kernel(
             for i in range(4):
                 c = 4 * hf + i
                 nc.tensor.transpose(bank[:, i, :], g_pick[nt][:, c * CH : (c + 1) * CH], ident[:])
-            sq = keep.tile([P, 4, P], F32, name=f"g_sq{nt}{hf}")
+            sq = placed(f"g_sq{nt}{hf}", 118 + 2 * (2 * nt + hf), [P, 4, P], F32)
             nc.scalar.activation(sq[:], bank[:], ACT.Square)
             g_sq[nt, hf] = sq
 
-        total = {}
-
-        def open_sum(nt, hf, b):
+        def replace(nt, hf, b, kib):
             bank = bank_tile(f"sum{nt}{hf}", b, [P, 4, CH])
             for i in range(4):
                 nc.tensor.matmul(
                     bank[:, i, :], g_sq[nt, hf][:, i, :], ident[:], start=(i == 0), stop=False, is_transpose=True
                 )
-            total[nt, hf] = bank
-
-        def close_sum(nt, hf):
-            bank = total[nt, hf]
             for i in range(4):
                 nc.tensor.matmul(
                     bank[:, i, :],
@@ -297,69 +300,72 @@ def tile_list_sauce_seasoning_kernel(
                     stop=(i == 3),
                     is_transpose=True,
                 )
-            new = ring.tile([P, HALF], F32, name="root", bufs=3)
+            new = placed(f"root{nt}{hf}", kib, [P, HALF], F32)
             nc.scalar.activation(new[:], bank[:].rearrange("p i j -> p (i j)"), ACT.Sqrt)
-            root[nt, hf] = new
+            nc.vector.tensor_copy(page[nt][:].indirect(half_list(hf)), new[:])
 
-        def replace(nt, hf):
-            nc.vector.tensor_copy(page[nt][:].indirect(half_list(hf)), root[nt, hf][:])
-
-        pick_intensity(0, 74)
-        round_w1(0, 0, 44)
-        load_w1(1, 1, 0)
-        quantize_w1(0, 0, keep.tile([P, KP], U32, name="w1q00", align_bytes=64))
-        load_page(1, 44)
-        round_w1_half(0, 1, 0, 52, nc.vector.tensor_copy)
-        round_w1_half(0, 1, 1, 54, nc.vector.tensor_copy)
-        wo = placed("wo", 8, [P, 2, N], I32)
-        nc.sync.dma_start(wo[:], wo_words.rearrange("a p c i -> p a (c i)").bitcast(I32))
-        load_page(2, 12)
-        quantize_w1_half(0, 1, 0)
-        quantize_w1_half(0, 1, 1)
-        for c in range(NCH):
-            gates(0, c, 58 + 2 * c)
-        round_w1(1, 0, 118)
-        load_page(3, 23)
-        round_w1(1, 1, 122)
-        for c in range(NCH):
-            features(0, c)
+        round_w1(0, 0, nc.scalar.copy)
+        round_w1(0, 1, nc.vector.tensor_copy)
+        load_page(1, 0)
+        quantize_w1(0, 0)
+        quantize_w1(0, 1)
+        load_page(2, 152.5)
+        pick_intensity(0, 94)
+        for c in range(4):
+            gates(0, c, c, 16 + 2 * c)
+        for c, kib in enumerate((148.5, 150.5, 160.5, 162.5)):
+            gates(1, c, 4 + c, kib)
+        round_w1_aside(1, 0)
+        load_page(3, 37)
+        h00 = open_h([(0, c) for c in range(4)], 78)
+        h10 = open_h([(1, c) for c in range(4)], 86)
+        h_a = open_h([(0, 4), (0, 5), (1, 4), (1, 5)], 192)
+        h_b = open_h([(0, 6), (0, 7), (1, 6), (1, 7)], 180)
+        for c in range(4):
+            features(0, c, c)
             gate_features(0, c)
-        quantize_w1(1, 0, placed("w1q10", 72, [P, KP], U32))
-        pick_intensity(1, 116)
-        quantize_w1(1, 1, placed("w1q11", 120, [P, KP], U32))
-        quantize_h(0, 0, placed("hq0", 122, [P, S], U32))
-        for c in range(NCH):
-            gates(1, c, 2 * c if c < 4 else 118 + 2 * c)
-        for c in range(NCH):
-            features(1, c)
-        for c in range(5):
+        square_intensity(0, 0, 7)
+        round_w1(1, 1, nc.scalar.copy)
+        quantize_h(h00)
+        quantize_w1(1, 0)
+        quantize_w1(1, 1)
+        pick_intensity(1, 174)
+        for c in range(4, NCH):
+            gates(0, c, c, 20.5 + 2 * c)
+        for c in range(4):
+            features(1, c, 4 + c)
             gate_features(1, c)
-        square_intensity(0, 0, 3)
-        open_sum(0, 0, 4)
-        quantize_h(1, 0, keep.tile([P, HALF], U32, name="hq10", align_bytes=64))
-        pick_intensity(2, 108)
-        for c, b in enumerate((3, 2, 5, 6)):
-            seasoning(c, b)
-        close_sum(0, 0)
-        square_intensity(1, 0, 3)
-        open_sum(1, 0, 2)
-        close_sum(1, 0)
-        for c in range(5, NCH):
-            gate_features(1, c)
-        quantize_h(1, 1, keep.tile([P, HALF], U32, name="hq11", align_bytes=64))
-        pick_intensity(3, 112)
-        replace(0, 0)
-        replace(1, 0)
-        for nt, (b_square, b_sum) in ((2, (5, 6)), (3, (4, 2))):
-            square_intensity(nt, 0, b_square)
-            open_sum(nt, 0, b_sum)
-            close_sum(nt, 0)
-            replace(nt, 0)
-        for c, b in zip(range(4, NCH), (7, 0, 1, 7)):
-            seasoning(c, b)
-        for nt, (b_square, b_sum) in enumerate(((3, 5), (0, 6), (1, 4), (7, 2))):
-            square_intensity(nt, 1, b_square)
-            open_sum(nt, 1, b_sum)
-            close_sum(nt, 1)
-            replace(nt, 1)
+        quantize_h(h10)
+        for c in range(4):
+            seasoning(c, 4 + c)
+        pick_intensity(2, 86.5)
+        pick_intensity(3, 162.5)
+        for c in range(4, NCH):
+            gates(1, c, c - 4, 54 + 2 * c)
+        root_warm = kept("root_warm", [P, 1], F32)
+        nc.scalar.activation(root_warm[:], gate[1, NCH - 1][:, 0, 0:1], ACT.Sqrt)
+        for i, (rb, c) in enumerate(h_a[0]):
+            if i == 3:
+                replace(0, 0, 4, 134)
+            features(rb, c, (0, 1, 2, 5)[i])
+            gate_features_aside(rb, c, 110 + 2 * i)
+        quantize_h(h_a)
+        for i, (rb, c) in enumerate(h_b[0]):
+            if i == 2:
+                square_intensity(1, 0, 4)
+                replace(1, 0, 5, 136)
+            features(rb, c, (6, 7)[i % 2])
+            gate_features_aside(rb, c, 184 + 2 * i)
+        square_intensity(2, 0, 4)
+        seasoning(4, 6)
+        seasoning(5, 7)
+        quantize_h(h_b)
+        replace(2, 0, 0, 189)
+        square_intensity(3, 0, 5)
+        replace(3, 0, 1, 191)
+        seasoning(6, 2)
+        seasoning(7, 3)
+        for nt in range(4):
+            square_intensity(nt, 1, (4, 5)[nt % 2])
+            replace(nt, 1, (6, 7)[nt % 2], 140 + 2 * nt)
             nc.sync.dma_start(out[nt * P : (nt + 1) * P, :], page[nt][:])

@@ -91,7 +91,7 @@ def tile_list_sauce_seasoning_kernel(
             v_sc1[:].bitcast(I32).rearrange("p (r w) -> p r w", w=32),
             zero_a[:].unsqueeze(1).to_broadcast([P, 8, 32]),
         )
-        wg_sc_raw = placed("wg_sc_raw", 41, [P, 2, H], U8)
+        wg_sc_raw = placed("wg_sc_raw", 44, [P, 2, H], U8)
         nc.vector.tensor_copy(
             wg_sc_raw[:].bitcast(I32).rearrange("p a (r w) -> p (a r) w", w=32),
             zero_b[:].unsqueeze(1).to_broadcast([P, 16, 32]),
@@ -128,57 +128,41 @@ def tile_list_sauce_seasoning_kernel(
 
         v = {}
 
-        def gather_words(a, hf):
-            words = kept(f"v{a}{hf}", [P, HALF], U32)
+        def gather_words(a, hf, words):
             nc.vector.tensor_copy(words[:], tab[a][:].bitcast(U32).indirect(half_list(hf)))
             v[a, hf] = words
 
         def v_codes(a, c):
             return v[a, c // 4][:, c % 4 * CH : (c % 4 + 1) * CH].bitcast(FP8X4)
 
-        gather_words(0, 0)
-        gather_words(0, 1)
-        load_page(0, 8)
+        gather_words(0, 0, kept("v00", [P, HALF], U32))
         wg_sc = kept("wg_sc", [P, 2 * H], U8)
         nc.vector.tensor_copy(
             wg_sc[:].rearrange("p (g t m) -> p g t m", g=4, t=PACK),
             wg_sc_raw[:].rearrange("p a (g m t) -> p (a g) t m", g=2, t=PACK),
         )
-        load_w1(1, 0, 37)
-        gather_words(1, 0)
-        gather_words(1, 1)
+        load_page(0, 37)
+        gather_words(0, 1, placed("v01", 45, [P, HALF], U32))
+        load_w1(1, 0, 8)
+        gather_words(1, 0, kept("v10", [P, HALF], U32))
+        gather_words(1, 1, kept("v11", [P, HALF], U32))
         load_w1(1, 1, 28.5)
-        wo = placed("wo", 24, [P, 2, N], I32)
-        nc.sync.dma_start(wo[:], wo_words.rearrange("a p c i -> p a (c i)").bitcast(I32))
-        wo_sc = placed("wo_sc", 28, [P, N], U8)
-        nc.gpsimd.memset(wo_sc[:].bitcast(I32), 0)
-        load_packed_scales(wo_sc, wo_scales)
 
         w1_bf, w1q = {}, {}
 
         def round_w1(rb, a, copy):
-            grouped = placed(f"w1_bf{rb}{a}", (150, 160, 166, 174)[2 * rb + a], [P, PACK * KP], BF16)
+            grouped = placed(f"w1_bf{rb}{a}", (150, 160, 168, 174)[2 * rb + a], [P, PACK * KP], BF16)
             copy(
                 grouped[:].rearrange("p (t m e j) -> p m j e t", t=PACK, e=2, j=PACK),
                 w1_raw[rb, a][:].rearrange("p j (m e t) -> p m j e t", e=2, t=PACK),
             )
             w1_bf[rb, a] = grouped[:]
 
-        def round_w1_aside(rb, a):
-            grouped = placed(f"w1_bf{rb}{a}", 166, [P, PACK, P, PACK], BF16)
-            for u in range(2):
-                nc.gpsimd.tensor_scalar(
-                    grouped[:, 2 * u : 2 * u + 2, :, :],
-                    w1_raw[rb, a][:].rearrange("p j (m t) -> p t m j", t=PACK)[:, 2 * u : 2 * u + 2, :, :],
-                    1.0,
-                    0.0,
-                    ALU.mult,
-                    ALU.add,
-                )
-            w1_bf[rb, a] = grouped[:].rearrange("p t m j -> p (t m j)")
-
-        def quantize(name, src, width):
-            codes = kept(f"{name}_codes", [P, width], U32)
+        def quantize(name, src, width, kib=None):
+            if kib is None:
+                codes = kept(f"{name}_codes", [P, width], U32)
+            else:
+                codes = placed(f"{name}_codes", kib, [P, width], U32)
             scales = kept(f"{name}_scales", [P, width], U8)
             nc.vector.quantize_mx(out=codes[:].bitcast(FP8X4), scales=scales[:], in_=src)
             return [(codes[:, i : i + P], scales[:, i : i + P]) for i in range(0, width, P)]
@@ -188,23 +172,32 @@ def tile_list_sauce_seasoning_kernel(
 
         gate, feature, h_bf, hq = {}, {}, {}, {}
 
-        def gates(rb, c, b, kib):
-            bank = bank_tile(f"b{rb}{c}", b, [P, PACK, CH])
+        logits = {}
+
+        def gate_pass(rb, c, a, b):
+            if a == 0:
+                logits[rb, c] = bank_tile(f"b{rb}{c}", b, [P, PACK, CH])
             for t in range(PACK):
-                for a in range(2):
-                    col = a * H + rb * KP + t * P
-                    nc.tensor.matmul_mx(
-                        out=bank[:, t, :],
-                        lhsT=wg[rb][:, 2 * (a * KP + t * P) : 2 * (a * KP + (t + 1) * P)].bitcast(FP4X4),
-                        lhsT_scale=wg_sc[:, col : col + P],
-                        rhs=v_codes(a, c),
-                        rhs_scale=v_planes[a][:, c * CH : (c + 1) * CH],
-                        start=(a == 0),
-                        stop=(a == 1),
-                    )
+                col = a * H + rb * KP + t * P
+                nc.tensor.matmul_mx(
+                    out=logits[rb, c][:, t, :],
+                    lhsT=wg[rb][:, 2 * (a * KP + t * P) : 2 * (a * KP + (t + 1) * P)].bitcast(FP4X4),
+                    lhsT_scale=wg_sc[:, col : col + P],
+                    rhs=v_codes(a, c),
+                    rhs_scale=v_planes[a][:, c * CH : (c + 1) * CH],
+                    start=(a == 0 and t == 0),
+                    stop=(a == 1 and t == PACK - 1),
+                )
+
+        def sigmoid(rb, c, kib):
             sig = placed(f"gate{rb}{c}", kib, [P, CH, PACK], F32)
-            nc.scalar.activation(sig[:], bank[:].rearrange("p t j -> p j t"), ACT.Sigmoid)
+            nc.scalar.activation(sig[:], logits[rb, c][:].rearrange("p t j -> p j t"), ACT.Sigmoid)
             gate[rb, c] = sig
+
+        def gates(rb, c, b, kib):
+            gate_pass(rb, c, 0, b)
+            gate_pass(rb, c, 1, b)
+            sigmoid(rb, c, kib)
 
         def features(rb, c, b):
             bank = bank_tile(f"a{rb}{c}", b, [P, PACK, CH])
@@ -246,9 +239,9 @@ def tile_list_sauce_seasoning_kernel(
                 ALU.mult,
             )
 
-        def quantize_h(group):
+        def quantize_h(group, kib=None):
             parts, rows = group
-            made = quantize(f"hq{parts[0][0]}{parts[0][1]}", rows[:], len(parts) * CH)
+            made = quantize(f"hq{parts[0][0]}{parts[0][1]}", rows[:], len(parts) * CH, kib)
             for part, operand in zip(parts, made):
                 hq[part] = operand
 
@@ -285,87 +278,110 @@ def tile_list_sauce_seasoning_kernel(
             nc.scalar.activation(sq[:], bank[:], ACT.Square)
             g_sq[nt, hf] = sq
 
-        def replace(nt, hf, b, kib):
-            bank = bank_tile(f"sum{nt}{hf}", b, [P, 4, CH])
-            for i in range(4):
+        def replace(nt, first, count, b, kib):
+            bank = bank_tile(f"sum{nt}{first}", b, [P, count, CH])
+            for i in range(count):
+                c = first + i
                 nc.tensor.matmul(
-                    bank[:, i, :], g_sq[nt, hf][:, i, :], ident[:], start=(i == 0), stop=False, is_transpose=True
+                    bank[:, i, :], g_sq[nt, c // 4][:, c % 4, :], ident[:], start=(i == 0), stop=False, is_transpose=True
                 )
-            for i in range(4):
+            for i in range(count):
                 nc.tensor.matmul(
                     bank[:, i, :],
-                    y_sq[4 * hf + i][:, nt * P : (nt + 1) * P],
+                    y_sq[first + i][:, nt * P : (nt + 1) * P],
                     ident[:],
                     start=False,
-                    stop=(i == 3),
+                    stop=(i == count - 1),
                     is_transpose=True,
                 )
-            new = placed(f"root{nt}{hf}", kib, [P, HALF], F32)
+            new = placed(f"root{nt}{first}", kib, [P, count * CH], F32)
             nc.scalar.activation(new[:], bank[:].rearrange("p i j -> p (i j)"), ACT.Sqrt)
-            nc.vector.tensor_copy(page[nt][:].indirect(half_list(hf)), new[:])
+            part = offsets[:, first * (CH // 16) : (first + count) * (CH // 16)]
+            nc.vector.tensor_copy(page[nt][:].indirect(part), new[:])
+
+        def store(nt):
+            nc.sync.dma_start(out[nt * P : (nt + 1) * P, :], page[nt][:])
 
         round_w1(0, 0, nc.scalar.copy)
         round_w1(0, 1, nc.vector.tensor_copy)
         load_page(1, 0)
         quantize_w1(0, 0)
+        wo = placed("wo", 153, [P, 2, N], I32)
+        nc.sync.dma_start(wo[:], wo_words.rearrange("a p c i -> p a (c i)").bitcast(I32))
+        wo_sc = placed("wo_sc", 152.5, [P, N], U8)
+        nc.gpsimd.memset(wo_sc[:].bitcast(I32), 0)
+        load_packed_scales(wo_sc, wo_scales)
         quantize_w1(0, 1)
-        load_page(2, 152.5)
         pick_intensity(0, 94)
+        for rb in range(2):
+            for c in range(4):
+                gate_pass(rb, c, 0, 4 * rb + c)
         for c in range(4):
-            gates(0, c, c, 16 + 2 * c)
+            gate_pass(0, c, 1, c)
+            sigmoid(0, c, 16 + 2 * c)
         for c, kib in enumerate((148.5, 150.5, 160.5, 162.5)):
-            gates(1, c, 4 + c, kib)
-        round_w1_aside(1, 0)
-        load_page(3, 37)
+            gate_pass(1, c, 1, 4 + c)
+            sigmoid(1, c, kib)
+        round_w1(1, 0, nc.scalar.copy)
+        load_page(2, 8)
         h00 = open_h([(0, c) for c in range(4)], 78)
         h10 = open_h([(1, c) for c in range(4)], 86)
         h_a = open_h([(0, 4), (0, 5), (1, 4), (1, 5)], 192)
-        h_b = open_h([(0, 6), (0, 7), (1, 6), (1, 7)], 180)
+        h_b_parts = [(0, 6), (0, 7), (1, 6), (1, 7)]
         for c in range(4):
-            features(0, c, c)
+            features(0, c, 4 + c)
             gate_features(0, c)
-        square_intensity(0, 0, 7)
         round_w1(1, 1, nc.scalar.copy)
         quantize_h(h00)
+        load_page(3, 74)
         quantize_w1(1, 0)
         quantize_w1(1, 1)
-        pick_intensity(1, 174)
+        pick_intensity(1, 175)
         for c in range(4, NCH):
-            gates(0, c, c, 20.5 + 2 * c)
+            gates(0, c, c - 4, 20.5 + 2 * c)
         for c in range(4):
-            features(1, c, 4 + c)
+            features(1, c, c)
             gate_features(1, c)
         quantize_h(h10)
-        for c in range(4):
-            seasoning(c, 4 + c)
         pick_intensity(2, 86.5)
         pick_intensity(3, 162.5)
         for c in range(4, NCH):
-            gates(1, c, c - 4, 54 + 2 * c)
+            gates(1, c, c, 159 + 2 * c)
         root_warm = kept("root_warm", [P, 1], F32)
         nc.scalar.activation(root_warm[:], gate[1, NCH - 1][:, 0, 0:1], ACT.Sqrt)
+        square_intensity(0, 0, 4)
         for i, (rb, c) in enumerate(h_a[0]):
-            if i == 3:
-                replace(0, 0, 4, 134)
-            features(rb, c, (0, 1, 2, 5)[i])
-            gate_features_aside(rb, c, 110 + 2 * i)
+            features(rb, c, (5, 6, 7, 4)[i])
+        for c in range(4):
+            seasoning(c, c)
+        replace(0, 0, 4, 0, 134)
+        for i, (rb, c) in enumerate(h_a[0]):
+            gate_features_aside(rb, c, 184 + 2 * i)
         quantize_h(h_a)
+        square_intensity(1, 0, 1)
+        replace(1, 0, 4, 2, 190)
+        h_b = open_h(h_b_parts, 192)
         for i, (rb, c) in enumerate(h_b[0]):
             if i == 2:
-                square_intensity(1, 0, 4)
-                replace(1, 0, 5, 136)
-            features(rb, c, (6, 7)[i % 2])
-            gate_features_aside(rb, c, 184 + 2 * i)
-        square_intensity(2, 0, 4)
-        seasoning(4, 6)
-        seasoning(5, 7)
-        quantize_h(h_b)
-        replace(2, 0, 0, 189)
-        square_intensity(3, 0, 5)
-        replace(3, 0, 1, 191)
-        seasoning(6, 2)
-        seasoning(7, 3)
-        for nt in range(4):
-            square_intensity(nt, 1, (4, 5)[nt % 2])
-            replace(nt, 1, (6, 7)[nt % 2], 140 + 2 * nt)
-            nc.sync.dma_start(out[nt * P : (nt + 1) * P, :], page[nt][:])
+                square_intensity(2, 0, 1)
+                replace(2, 0, 4, 2, 136)
+            features(rb, c, (3, 0, 5, 6)[i])
+            gate_features_aside(rb, c, 62 + 2 * i if i < 3 else 138)
+        seasoning(4, 5)
+        seasoning(5, 6)
+        quantize_h(h_b, 136)
+        square_intensity(3, 0, 4)
+        replace(3, 0, 4, 7, 138)
+        square_intensity(0, 1, 1)
+        replace(0, 4, 2, 2, 192)
+        square_intensity(1, 1, 4)
+        replace(1, 4, 2, 5, 193)
+        seasoning(6, 7)
+        seasoning(7, 2)
+        for nt in range(2):
+            replace(nt, 6, 2, (6, 3)[nt], 142 + nt)
+            store(nt)
+        for nt in range(2, 4):
+            square_intensity(nt, 1, (1, 4)[nt % 2])
+            replace(nt, 4, 4, (0, 5)[nt % 2], 140 + 2 * nt)
+            store(nt)

@@ -21,9 +21,14 @@ P = 128
 PACK = 4
 KP = P * PACK
 CH = 128
-NCH = S // CH
-HALF = 512
+GR = 2 * CH
 KIB = 1024
+
+SLOT_A, SLOT_B, SLOT_C = 0, 8, 16
+ROUNDED = (24, 28, 32, 37)
+WO_SCALES, WO_WORDS, H_ROWS, PAGE3 = 32, 32.5, 36.5, 40.5
+GATES, PLAIN, Y_SQ, G_SQ, PICK1 = 49, 81, 113, 129, 147
+FIRST_ROOT = 159
 
 
 def tile_list_sauce_seasoning_kernel(
@@ -47,15 +52,27 @@ def tile_list_sauce_seasoning_kernel(
         offsets = keep.tile([P, S // 16], U16, name="offsets")
         nc.sync.dma_start(offsets[:], offs)
 
-        def half_list(hf):
-            return offsets[:, hf * (HALF // 16) : (hf + 1) * (HALF // 16)]
+        def listed(first, count):
+            return offsets[:, first * (CH // 16) : (first + count) * (CH // 16)]
 
-        def load_packed_scales(plane, src):
-            for q in range(4):
-                nc.sync.dma_start(
-                    plane[32 * q : 32 * q + 8, :].bitcast(I32),
-                    src[:, 4 * q : 4 * q + 4, :].bitcast(I32),
-                )
+        wg_raw = kept("wg_raw", [P, 2, 2 * H], U8)
+        nc.sync.dma_start(wg_raw[:].bitcast(I32), wg_words.rearrange("a p b -> p a b").bitcast(I32))
+        wg_sc_raw = placed("wg_sc_raw", SLOT_B, [P, KP], U8)
+        nc.sync.dma_start(wg_sc_raw[0:64, :].bitcast(I32), wg_scales.rearrange("a g (b c) -> (g b) a c", b=2).bitcast(I32))
+        tab_sc = placed("tab_sc", SLOT_C, [P, T], U8)
+        nc.vector.memset(tab_sc[:].bitcast(I32), 0)
+        for q in range(4):
+            nc.sync.dma_start(
+                tab_sc[32 * q : 32 * q + 4, :].bitcast(I32), tab_scales[0, 4 * q : 4 * q + 4, :].bitcast(I32)
+            )
+        nc.sync.dma_start(tab_sc[8:24, :].bitcast(I32), tab_scales[1].bitcast(I32))
+        zeros = placed("zeros", SLOT_A, [P, 32], I32)
+        nc.gpsimd.memset(zeros[:], 0)
+        wg_sc = kept("wg_sc", [P, 2 * H], U8)
+        nc.vector.tensor_copy(
+            wg_sc[:].bitcast(I32).rearrange("p (r w) -> p r w", w=32), zeros[:].unsqueeze(1).to_broadcast([P, 16, 32])
+        )
+        nc.vector.memset(wg_sc_raw[64:P, :].bitcast(I32), 0)
 
         tab, w1_raw, page = {}, {}, {}
 
@@ -77,86 +94,43 @@ def tile_list_sauce_seasoning_kernel(
             nc.sync.dma_start(rows[:], gT[nt * P : (nt + 1) * P, :])
             page[nt] = rows
 
-        wg_raw = placed("wg_raw", 37, [P, 2, 2 * H], U8)
-        nc.sync.dma_start(wg_raw[:].bitcast(I32), wg_words.rearrange("a p b -> p a b").bitcast(I32))
-        tab_sc = placed("tab_sc", 0, [P, T], U8)
-        nc.vector.memset(tab_sc[:].bitcast(I32), 0)
-        load_packed_scales(tab_sc, tab_scales)
-        zero_a = placed("zero_a", 8, [P, 32], I32)
-        nc.gpsimd.memset(zero_a[:], 0)
-        zero_b = placed("zero_b", 24 - 1 / 16, [P, 32], I32)
-        nc.gpsimd.memset(zero_b[:], 0)
+        load_words(0, SLOT_A)
         v_sc1 = kept("v_sc1", [P, S], U8)
-        nc.vector.tensor_copy(
-            v_sc1[:].bitcast(I32).rearrange("p (r w) -> p r w", w=32),
-            zero_a[:].unsqueeze(1).to_broadcast([P, 8, 32]),
-        )
-        wg_sc_raw = placed("wg_sc_raw", 44, [P, 2, H], U8)
-        nc.vector.tensor_copy(
-            wg_sc_raw[:].bitcast(I32).rearrange("p a (r w) -> p (a r) w", w=32),
-            zero_b[:].unsqueeze(1).to_broadcast([P, 16, 32]),
-        )
-        load_words(0, 8)
-        for q in range(4):
-            nc.sync.dma_start(
-                wg_sc_raw[32 * q : 32 * q + 4, :, :].bitcast(I32),
-                wg_scales[:, 4 * q : 4 * q + 4, :].rearrange("a r h -> r a h").bitcast(I32),
-            )
-        load_words(1, 24)
-        load_w1(0, 0, 16)
-
-        wg = {}
-        for rb in range(2):
-            block = kept(f"wg{rb}", [P, 2 * 2 * KP], U8)
-            nc.vector.tensor_copy(
-                block[:].bitcast(U16).rearrange("p (a t m) -> p a t m", a=2, t=PACK),
-                wg_raw[:].bitcast(U16)[:, :, rb * KP : (rb + 1) * KP].rearrange("p a (m t) -> p a t m", t=PACK),
-            )
-            wg[rb] = block
-        v_sc = kept("v_sc", [P, S], U8)
-        nc.vector.tensor_copy(v_sc[:], tab_sc[:].indirect(offsets[:]))
-        for q in range(4):
-            nc.sync.dma_start(
-                v_sc1[32 * q : 32 * q + 4, :].bitcast(I32), v_sc[32 * q + 4 : 32 * q + 8, :].bitcast(I32)
-            )
-        v_planes = [v_sc, v_sc1]
+        nc.vector.memset(v_sc1[:].bitcast(I32), 0)
         ident = kept("ident", [P, P], F32)
         make_identity(nc, ident[:])
         table_warm = kept("table_warm", [P, 1], F32)
         nc.scalar.activation(table_warm[:], ident[:, 0:1], ACT.Sigmoid)
-        load_w1(0, 1, 0)
 
-        v = {}
-
-        def gather_words(a, hf, words):
-            nc.vector.tensor_copy(words[:], tab[a][:].bitcast(U32).indirect(half_list(hf)))
-            v[a, hf] = words
-
-        def v_codes(a, c):
-            return v[a, c // 4][:, c % 4 * CH : (c % 4 + 1) * CH].bitcast(FP8X4)
-
-        gather_words(0, 0, kept("v00", [P, HALF], U32))
-        wg_sc = kept("wg_sc", [P, 2 * H], U8)
+        wg_sc_dealt = kept("wg_sc_dealt", [P, KP], U8)
         nc.vector.tensor_copy(
-            wg_sc[:].rearrange("p (g t m) -> p g t m", g=4, t=PACK),
-            wg_sc_raw[:].rearrange("p a (g m t) -> p (a g) t m", g=2, t=PACK),
+            wg_sc_dealt[:].rearrange("p (t m) -> p t m", t=PACK), wg_sc_raw[:].rearrange("p (m t) -> p t m", t=PACK)
         )
-        load_page(0, 37)
-        gather_words(0, 1, placed("v01", 45, [P, HALF], U32))
-        load_w1(1, 0, 8)
-        gather_words(1, 0, kept("v10", [P, HALF], U32))
-        gather_words(1, 1, kept("v11", [P, HALF], U32))
-        load_w1(1, 1, 28.5)
-
-        w1_bf, w1q = {}, {}
-
-        def round_w1(rb, a, copy):
-            grouped = placed(f"w1_bf{rb}{a}", (150, 160, 168, 174)[2 * rb + a], [P, PACK * KP], BF16)
-            copy(
-                grouped[:].rearrange("p (t m e j) -> p m j e t", t=PACK, e=2, j=PACK),
-                w1_raw[rb, a][:].rearrange("p j (m e t) -> p m j e t", e=2, t=PACK),
+        for q in range(4):
+            nc.sync.dma_start(wg_sc[32 * q : 32 * q + 4, :].bitcast(I32), wg_sc_dealt[16 * q : 16 * q + 16, :].bitcast(I32))
+        load_words(1, SLOT_B)
+        wg = {}
+        for rb in range(2):
+            block = kept(f"wg{rb}", [P, 2 * 2 * KP], U8)
+            nc.scalar.copy(
+                block[:].bitcast(U16).rearrange("p (a t m) -> p a t m", a=2, t=PACK),
+                wg_raw[:].bitcast(U16)[:, :, rb * KP : (rb + 1) * KP].rearrange("p a (m t) -> p a t m", t=PACK),
             )
-            w1_bf[rb, a] = grouped[:]
+            wg[rb] = block
+        v_sc_picked = kept("v_sc_picked", [P, S], U8)
+        nc.vector.tensor_copy(v_sc_picked[:], tab_sc[:].indirect(offsets[:]))
+        for q in range(4):
+            nc.sync.dma_start(
+                v_sc1[32 * q : 32 * q + 4, :].bitcast(I32), v_sc_picked[8 + 4 * q : 12 + 4 * q, :].bitcast(I32)
+            )
+        v_planes = (v_sc_picked, v_sc1)
+        load_w1(0, 0, SLOT_C)
+        v = {}
+        for a in range(2):
+            for hf in range(2):
+                v[a, hf] = kept(f"v{a}{hf}", [P, S // 2], U32)
+                nc.vector.tensor_copy(v[a, hf][:], tab[a][:].bitcast(U32).indirect(listed(4 * hf, 4)))
+            load_w1(a, 1 - a, (SLOT_A, SLOT_B)[a])
 
         def quantize(name, src, width, kib=None):
             if kib is None:
@@ -167,102 +141,158 @@ def tile_list_sauce_seasoning_kernel(
             nc.vector.quantize_mx(out=codes[:].bitcast(FP8X4), scales=scales[:], in_=src)
             return [(codes[:, i : i + P], scales[:, i : i + P]) for i in range(0, width, P)]
 
+        w1_bf, w1q = {}, {}
+
+        def round_w1(rb, a):
+            grouped = placed(f"w1_bf{rb}{a}", ROUNDED[2 * rb + a], [P, PACK * KP], BF16)
+            nc.vector.tensor_copy(
+                grouped[:].rearrange("p (t m e j) -> p m j e t", t=PACK, e=2, j=PACK),
+                w1_raw[rb, a][:].rearrange("p j (m e t) -> p m j e t", e=2, t=PACK),
+            )
+            w1_bf[rb, a] = grouped[:]
+
         def quantize_w1(rb, a):
             w1q[rb, a] = quantize(f"w1q{rb}{a}", w1_bf[rb, a], KP)
 
-        gate, feature, h_bf, hq = {}, {}, {}, {}
+        round_w1(0, 0)
+        load_w1(1, 1, SLOT_C)
+        quantize_w1(0, 0)
+        round_w1(0, 1)
+        load_page(0, SLOT_A)
+        quantize_w1(0, 1)
+        round_w1(1, 0)
+        load_page(1, SLOT_B)
+        quantize_w1(1, 0)
+        wo = placed("wo", WO_WORDS, [P, 2, N], I32)
+        nc.sync.dma_start(wo[:], wo_words.rearrange("a p c i -> p a (c i)").bitcast(I32))
+        wo_sc = placed("wo_sc", WO_SCALES, [P, N], U8)
+        nc.gpsimd.memset(wo_sc[:].bitcast(I32), 0)
+        for q in range(4):
+            nc.sync.dma_start(
+                wo_sc[32 * q : 32 * q + 8, :].bitcast(I32), wo_scales[:, 4 * q : 4 * q + 4, :].bitcast(I32)
+            )
+        round_w1(1, 1)
+        load_page(2, SLOT_C)
+        quantize_w1(1, 1)
+        load_page(3, PAGE3)
 
-        logits = {}
+        logits, gate, plain, hq, h_rows = {}, {}, {}, {}, {}
 
-        def gate_pass(rb, c, a, b):
+        def moving(a, first, width):
+            col = first % (S // 2)
+            return {
+                "rhs": v[a, first // (S // 2)][:, col : col + width].bitcast(FP8X4),
+                "rhs_scale": v_planes[a][:, first : first + width],
+            }
+
+        def gate_place(g, rb):
+            return PICK1 - 2 + 4 * rb if g == 0 else GATES + 4 * (2 * g + rb)
+
+        def plain_place(g, rb):
+            return PICK1 + 6 if g == 0 else PLAIN + 4 * (2 * g + rb)
+
+        def gate_pass(g, rb, u, a):
             if a == 0:
-                logits[rb, c] = bank_tile(f"b{rb}{c}", b, [P, PACK, CH])
-            for t in range(PACK):
-                col = a * H + rb * KP + t * P
+                logits[g, rb, u] = bank_tile(f"b{g}{rb}{u}", 4 * rb + 2 * (g % 2) + u, [P, 2, GR])
+            for e in range(2):
+                t = 2 * u + e
+                col = rb * H + a * KP + t * P
                 nc.tensor.matmul_mx(
-                    out=logits[rb, c][:, t, :],
+                    out=logits[g, rb, u][:, e, :],
                     lhsT=wg[rb][:, 2 * (a * KP + t * P) : 2 * (a * KP + (t + 1) * P)].bitcast(FP4X4),
                     lhsT_scale=wg_sc[:, col : col + P],
-                    rhs=v_codes(a, c),
-                    rhs_scale=v_planes[a][:, c * CH : (c + 1) * CH],
-                    start=(a == 0 and t == 0),
-                    stop=(a == 1 and t == PACK - 1),
+                    start=(a == 0 and e == 0),
+                    stop=(a == 1 and e == 1),
+                    **moving(a, g * GR, GR),
                 )
 
-        def sigmoid(rb, c, kib):
-            sig = placed(f"gate{rb}{c}", kib, [P, CH, PACK], F32)
-            nc.scalar.activation(sig[:], logits[rb, c][:].rearrange("p t j -> p j t"), ACT.Sigmoid)
-            gate[rb, c] = sig
+        def sigmoid(g, rb, u):
+            if u == 0:
+                gate[g, rb] = placed(f"gate{g}{rb}", gate_place(g, rb), [P, 2, GR, 2], F32)
+            nc.scalar.activation(gate[g, rb][:, u], logits[g, rb, u][:].rearrange("p e j -> p j e"), ACT.Sigmoid)
 
-        def gates(rb, c, b, kib):
-            gate_pass(rb, c, 0, b)
-            gate_pass(rb, c, 1, b)
-            sigmoid(rb, c, kib)
+        def gates(g, rb):
+            for u in range(2):
+                gate_pass(g, rb, u, 0)
+                gate_pass(g, rb, u, 1)
+                sigmoid(g, rb, u)
 
-        def features(rb, c, b):
-            bank = bank_tile(f"a{rb}{c}", b, [P, PACK, CH])
+        def feature_passes(dst, rb, t, first, width):
+            for a in range(2):
+                wc, ws = w1q[rb, a][t]
+                nc.tensor.matmul_mx(
+                    out=dst,
+                    lhsT=wc.bitcast(FP8X4),
+                    lhsT_scale=ws,
+                    start=(a == 0),
+                    stop=(a == 1),
+                    **moving(a, first, width),
+                )
+
+        def features(g, rb, banks):
+            copied = placed(f"a_plain{g}{rb}", plain_place(g, rb), [P, 2, GR, 2], F32)
+            for u in range(2):
+                bank = bank_tile(f"a{g}{rb}{u}", banks[u], [P, 2, GR])
+                for e in range(2):
+                    feature_passes(bank[:, e, :], rb, 2 * u + e, g * GR, GR)
+                nc.scalar.copy(copied[:, u], bank[:].rearrange("p e j -> p j e"))
+            plain[g, rb] = copied
+
+        def chunk_features(rb, c, b):
+            bank = bank_tile(f"a_chunk{rb}{c}", b, [P, PACK, CH])
             for t in range(PACK):
-                for a in range(2):
-                    wc, ws = w1q[rb, a][t]
-                    nc.tensor.matmul_mx(
-                        out=bank[:, t, :],
-                        lhsT=wc.bitcast(FP8X4),
-                        lhsT_scale=ws,
-                        rhs=v_codes(a, c),
-                        rhs_scale=v_sc[4 * a : P, c * CH : (c + 1) * CH],
-                        start=(a == 0),
-                        stop=(a == 1),
-                    )
-            feature[rb, c] = bank
+                feature_passes(bank[:, t, :], rb, t, c * CH, CH)
+            return bank
 
-        def open_h(parts, kib):
-            rows = placed(f"h_bf{parts[0][0]}{parts[0][1]}", kib, [P, len(parts) * KP], BF16)
-            for i, part in enumerate(parts):
-                h_bf[part] = rows[:, i * KP : (i + 1) * KP]
-            return parts, rows
+        def open_h(g):
+            h_rows[g] = placed(f"h_bf{g}", H_ROWS, [P, 2, GR, 2, 2], BF16)
 
-        def gate_features(rb, c):
-            nc.vector.tensor_tensor(
-                h_bf[rb, c].rearrange("p (j t) -> p j t", t=PACK),
-                feature[rb, c][:].rearrange("p t j -> p j t"),
-                gate[rb, c][:],
-                ALU.mult,
-            )
-
-        def gate_features_aside(rb, c, kib):
-            plain = placed(f"a_plain{rb}{c}", kib, [P, CH, PACK], F32)
-            nc.scalar.copy(plain[:], feature[rb, c][:].rearrange("p t j -> p j t"))
+        def gate_features(g, rb):
             nc.gpsimd.tensor_tensor(
-                h_bf[rb, c],
-                plain[:].rearrange("p j t -> p (j t)"),
-                gate[rb, c][:].rearrange("p j t -> p (j t)"),
+                h_rows[g][:, rb],
+                plain[g, rb][:].rearrange("p u j e -> p j u e"),
+                gate[g, rb][:].rearrange("p u j e -> p j u e"),
                 ALU.mult,
             )
 
-        def quantize_h(group, kib=None):
-            parts, rows = group
-            made = quantize(f"hq{parts[0][0]}{parts[0][1]}", rows[:], len(parts) * CH, kib)
-            for part, operand in zip(parts, made):
-                hq[part] = operand
+        def gate_chunk(rb, c, bank):
+            cols = slice(c % 2 * CH, (c % 2 + 1) * CH)
+            nc.vector.tensor_tensor(
+                h_rows[c // 2][:, rb, cols],
+                bank[:].rearrange("p (u e) j -> p j u e", e=2),
+                gate[c // 2, rb][:, :, cols, :].rearrange("p u j e -> p j u e"),
+                ALU.mult,
+            )
+
+        def gate_group(g):
+            open_h(g)
+            gate_features(g, 0)
+            gate_features(g, 1)
 
         y_sq, g_pick, g_sq = {}, {}, {}
 
-        def seasoning(c, b):
-            bank = bank_tile(f"y{c}", b, [P, N])
-            for rb in range(2):
-                codes, scales = hq[rb, c]
-                nc.tensor.matmul_mx(
-                    out=bank[:],
-                    lhsT=codes.bitcast(FP8X4),
-                    lhsT_scale=scales,
-                    rhs=wo[:, rb, :].bitcast(FP8X4),
-                    rhs_scale=wo_sc[4 * rb : P, :],
-                    start=(rb == 0),
-                    stop=(rb == 1),
-                )
-            sq = placed(f"y_sq{c}", 102 + 2 * c, [P, N], F32)
-            nc.scalar.activation(sq[:], bank[:], ACT.Square)
-            y_sq[c] = sq
+        def quantize_h(g, kib=None):
+            made = quantize(f"hq{g}", h_rows[g][:].rearrange("p r j u e -> p (r j u e)"), 2 * GR, kib)
+            for i, operand in enumerate(made):
+                hq[i // 2, 2 * g + i % 2] = operand
+
+        def seasoning(g):
+            for c in (2 * g, 2 * g + 1):
+                bank = bank_tile(f"y{c}", 4 + c % 2, [P, N])
+                for rb in range(2):
+                    codes, scales = hq[rb, c]
+                    nc.tensor.matmul_mx(
+                        out=bank[:],
+                        lhsT=codes.bitcast(FP8X4),
+                        lhsT_scale=scales,
+                        rhs=wo[:, rb, :].bitcast(FP8X4),
+                        rhs_scale=wo_sc[4 * rb : P, :],
+                        start=(rb == 0),
+                        stop=(rb == 1),
+                    )
+                sq = placed(f"y_sq{c}", Y_SQ + 2 * c, [P, N], F32)
+                nc.scalar.activation(sq[:], bank[:], ACT.Square)
+                y_sq[c] = sq
 
         def pick_intensity(nt, kib):
             picked = placed(f"g_pick{nt}", kib, [P, S], F32)
@@ -274,11 +304,15 @@ def tile_list_sauce_seasoning_kernel(
             for i in range(4):
                 c = 4 * hf + i
                 nc.tensor.transpose(bank[:, i, :], g_pick[nt][:, c * CH : (c + 1) * CH], ident[:])
-            sq = placed(f"g_sq{nt}{hf}", 118 + 2 * (2 * nt + hf), [P, 4, P], F32)
+            sq = placed(f"g_sq{nt}{hf}", G_SQ + 2 * (2 * nt + hf), [P, 4, P], F32)
             nc.scalar.activation(sq[:], bank[:], ACT.Square)
             g_sq[nt, hf] = sq
 
-        def replace(nt, first, count, b, kib):
+        def roots(name, kib, count):
+            rows = placed(name, kib, [P, count, GR], F32)
+            return [rows[:, i, :] for i in range(count)]
+
+        def replace(nt, first, count, b, new):
             bank = bank_tile(f"sum{nt}{first}", b, [P, count, CH])
             for i in range(count):
                 c = first + i
@@ -294,94 +328,78 @@ def tile_list_sauce_seasoning_kernel(
                     stop=(i == count - 1),
                     is_transpose=True,
                 )
-            new = placed(f"root{nt}{first}", kib, [P, count * CH], F32)
-            nc.scalar.activation(new[:], bank[:].rearrange("p i j -> p (i j)"), ACT.Sqrt)
-            part = offsets[:, first * (CH // 16) : (first + count) * (CH // 16)]
-            nc.vector.tensor_copy(page[nt][:].indirect(part), new[:])
+            nc.scalar.activation(new, bank[:].rearrange("p i j -> p (i j)"), ACT.Sqrt)
+            nc.vector.tensor_copy(page[nt][:].indirect(listed(first, count)), new)
 
         def store(nt):
             nc.sync.dma_start(out[nt * P : (nt + 1) * P, :], page[nt][:])
 
-        round_w1(0, 0, nc.scalar.copy)
-        round_w1(0, 1, nc.vector.tensor_copy)
-        load_page(1, 0)
-        quantize_w1(0, 0)
-        wo = placed("wo", 153, [P, 2, N], I32)
-        nc.sync.dma_start(wo[:], wo_words.rearrange("a p c i -> p a (c i)").bitcast(I32))
-        wo_sc = placed("wo_sc", 152.5, [P, N], U8)
-        nc.gpsimd.memset(wo_sc[:].bitcast(I32), 0)
-        load_packed_scales(wo_sc, wo_scales)
-        quantize_w1(0, 1)
-        pick_intensity(0, 94)
-        for rb in range(2):
-            for c in range(4):
-                gate_pass(rb, c, 0, 4 * rb + c)
-        for c in range(4):
-            gate_pass(0, c, 1, c)
-            sigmoid(0, c, 16 + 2 * c)
-        for c, kib in enumerate((148.5, 150.5, 160.5, 162.5)):
-            gate_pass(1, c, 1, 4 + c)
-            sigmoid(1, c, kib)
-        round_w1(1, 0, nc.scalar.copy)
-        load_page(2, 8)
-        h00 = open_h([(0, c) for c in range(4)], 78)
-        h10 = open_h([(1, c) for c in range(4)], 86)
-        h_a = open_h([(0, 4), (0, 5), (1, 4), (1, 5)], 192)
-        h_b_parts = [(0, 6), (0, 7), (1, 6), (1, 7)]
-        for c in range(4):
-            features(0, c, 4 + c)
-            gate_features(0, c)
-        round_w1(1, 1, nc.scalar.copy)
-        quantize_h(h00)
-        load_page(3, 74)
-        quantize_w1(1, 0)
-        quantize_w1(1, 1)
-        pick_intensity(1, 175)
-        for c in range(4, NCH):
-            gates(0, c, c - 4, 20.5 + 2 * c)
-        for c in range(4):
-            features(1, c, c)
-            gate_features(1, c)
-        quantize_h(h10)
-        pick_intensity(2, 86.5)
-        pick_intensity(3, 162.5)
-        for c in range(4, NCH):
-            gates(1, c, c, 159 + 2 * c)
+        first_half = [(g, rb, u) for rb in range(2) for g in range(2) for u in range(2)]
+        for g, rb, u in first_half:
+            gate_pass(g, rb, u, 0)
+        for g, rb, u in first_half:
+            gate_pass(g, rb, u, 1)
+            sigmoid(g, rb, u)
+        features(0, 0, (6, 7))
+        gates(2, 0)
+        gates(3, 0)
+        gates(2, 1)
+        gates(3, 1)
+        direct = [chunk_features(1, c, c) for c in range(2)]
+        features(1, 0, (2, 3))
         root_warm = kept("root_warm", [P, 1], F32)
-        nc.scalar.activation(root_warm[:], gate[1, NCH - 1][:, 0, 0:1], ACT.Sqrt)
-        square_intensity(0, 0, 4)
-        for i, (rb, c) in enumerate(h_a[0]):
-            features(rb, c, (5, 6, 7, 4)[i])
-        for c in range(4):
-            seasoning(c, c)
-        replace(0, 0, 4, 0, 134)
-        for i, (rb, c) in enumerate(h_a[0]):
-            gate_features_aside(rb, c, 184 + 2 * i)
-        quantize_h(h_a)
-        square_intensity(1, 0, 1)
-        replace(1, 0, 4, 2, 190)
-        h_b = open_h(h_b_parts, 192)
-        for i, (rb, c) in enumerate(h_b[0]):
-            if i == 2:
-                square_intensity(2, 0, 1)
-                replace(2, 0, 4, 2, 136)
-            features(rb, c, (3, 0, 5, 6)[i])
-            gate_features_aside(rb, c, 62 + 2 * i if i < 3 else 138)
-        seasoning(4, 5)
-        seasoning(5, 6)
-        quantize_h(h_b, 136)
-        square_intensity(3, 0, 4)
-        replace(3, 0, 4, 7, 138)
-        square_intensity(0, 1, 1)
-        replace(0, 4, 2, 2, 192)
-        square_intensity(1, 1, 4)
-        replace(1, 4, 2, 5, 193)
-        seasoning(6, 7)
-        seasoning(7, 2)
+        nc.scalar.activation(root_warm[:], gate[3, 1][:, 1, 0, 0:1], ACT.Sqrt)
+        pick_intensity(0, ROUNDED[0])
+        open_h(0)
+        gate_features(0, 0)
+        for c in range(2):
+            gate_chunk(1, c, direct[c])
+        features(1, 1, (0, 1))
+        quantize_h(0)
+        square_intensity(0, 0, 6)
+        seasoning(0)
+        pick_intensity(1, PICK1)
+        pick_intensity(2, PICK1 + 4)
+        new = roots("roots_a", FIRST_ROOT, 1)
+        replace(0, 0, 2, 6, new[0])
+        gate_group(1)
+        features(2, 0, (4, 5))
+        square_intensity(1, 0, 6)
+        features(2, 1, (4, 5))
+        quantize_h(1, FIRST_ROOT - 1.5)
+        pick_intensity(3, FIRST_ROOT + 0.5)
+        new = roots("roots_b", GATES + 1, 2)
+        replace(1, 0, 2, 7, new[0])
+        square_intensity(2, 0, 6)
+        replace(2, 0, 2, 0, new[1])
+        seasoning(1)
+        features(3, 0, (4, 5))
+        features(3, 1, (4, 5))
+        square_intensity(3, 0, 7)
+        gate_group(2)
+        quantize_h(2, GATES)
+        new = roots("roots_c", GATES + 2, 3)
+        replace(3, 0, 2, 1, new[0])
+        replace(0, 2, 2, 2, new[1])
+        replace(1, 2, 2, 3, new[2])
+        seasoning(2)
+        square_intensity(0, 1, 6)
+        square_intensity(1, 1, 7)
+        gate_group(3)
+        quantize_h(3, GATES + 2)
+        new = roots("roots_d", GATES + 4, 4)
+        replace(2, 2, 2, 0, new[0])
+        replace(3, 2, 2, 1, new[1])
+        replace(0, 4, 2, 6, new[2])
+        replace(1, 4, 2, 7, new[3])
+        seasoning(3)
+        square_intensity(2, 1, 2)
+        square_intensity(3, 1, 3)
+        new = roots("roots_e", PLAIN, 2)
         for nt in range(2):
-            replace(nt, 6, 2, (6, 3)[nt], 142 + nt)
+            replace(nt, 6, 2, nt, new[nt])
             store(nt)
         for nt in range(2, 4):
-            square_intensity(nt, 1, (1, 4)[nt % 2])
-            replace(nt, 4, 4, (0, 5)[nt % 2], 140 + 2 * nt)
+            last = placed(f"root_last{nt}", PLAIN + 2 * nt, [P, 2 * GR], F32)
+            replace(nt, 4, 4, nt, last[:])
             store(nt)

@@ -24,11 +24,11 @@ CH = 128
 GR = 2 * CH
 KIB = 1024
 
-SLOT_A, SLOT_B, SLOT_C = 0, 8, 16
-ROUNDED = (24, 28, 32, 37)
-WO_SCALES, WO_WORDS, H_ROWS, PAGE3 = 32, 32.5, 36.5, 40.5
-GATES, PLAIN, Y_SQ, G_SQ, PICK1 = 49, 81, 113, 129, 147
-FIRST_ROOT = 159
+SLOT_A, IDENT, SLOT_B, SLOT_C = 0, 8.5, 9, 17
+ROUNDED = (25, 29, 33, 38)
+WO_SCALES, WO_WORDS, H_ROWS, PAGE3 = 33, 33.5, 37.5, 41.5
+GATES, PLAIN, Y_SQ, G_SQ, PICK1 = 50, 82, 114, 130, 148
+FIRST_ROOT = 160
 
 
 def tile_list_sauce_seasoning_kernel(
@@ -57,7 +57,7 @@ def tile_list_sauce_seasoning_kernel(
 
         wg_raw = kept("wg_raw", [P, 2, 2 * H], U8)
         nc.sync.dma_start(wg_raw[:].bitcast(I32), wg_words.rearrange("a p b -> p a b").bitcast(I32))
-        wg_sc_raw = placed("wg_sc_raw", SLOT_B, [P, KP], U8)
+        wg_sc_raw = placed("wg_sc_raw", SLOT_B - 0.25, [P, KP], U8)
         nc.sync.dma_start(wg_sc_raw[0:64, :].bitcast(I32), wg_scales.rearrange("a g (b c) -> (g b) a c", b=2).bitcast(I32))
         tab_sc = placed("tab_sc", SLOT_C, [P, T], U8)
         nc.vector.memset(tab_sc[:].bitcast(I32), 0)
@@ -97,10 +97,9 @@ def tile_list_sauce_seasoning_kernel(
         load_words(0, SLOT_A)
         v_sc1 = kept("v_sc1", [P, S], U8)
         nc.vector.memset(v_sc1[:].bitcast(I32), 0)
-        ident = kept("ident", [P, P], F32)
-        make_identity(nc, ident[:])
         table_warm = kept("table_warm", [P, 1], F32)
-        nc.scalar.activation(table_warm[:], ident[:, 0:1], ACT.Sigmoid)
+        nc.gpsimd.memset(table_warm[:], 0.0)
+        nc.scalar.activation(table_warm[:], table_warm[:], ACT.Sigmoid)
 
         wg_sc_dealt = kept("wg_sc_dealt", [P, KP], U8)
         nc.vector.tensor_copy(
@@ -109,6 +108,8 @@ def tile_list_sauce_seasoning_kernel(
         for q in range(4):
             nc.sync.dma_start(wg_sc[32 * q : 32 * q + 4, :].bitcast(I32), wg_sc_dealt[16 * q : 16 * q + 16, :].bitcast(I32))
         load_words(1, SLOT_B)
+        ident = placed("ident", IDENT, [P, P], F32)
+        make_identity(nc, ident[:])
         wg = {}
         for rb in range(2):
             block = kept(f"wg{rb}", [P, 2 * 2 * KP], U8)
@@ -166,7 +167,7 @@ def tile_list_sauce_seasoning_kernel(
         wo = placed("wo", WO_WORDS, [P, 2, N], I32)
         nc.sync.dma_start(wo[:], wo_words.rearrange("a p c i -> p a (c i)").bitcast(I32))
         wo_sc = placed("wo_sc", WO_SCALES, [P, N], U8)
-        nc.gpsimd.memset(wo_sc[:].bitcast(I32), 0)
+        nc.vector.memset(wo_sc[:].bitcast(I32), 0)
         for q in range(4):
             nc.sync.dma_start(
                 wo_sc[32 * q : 32 * q + 8, :].bitcast(I32), wo_scales[:, 4 * q : 4 * q + 4, :].bitcast(I32)
@@ -378,28 +379,28 @@ def tile_list_sauce_seasoning_kernel(
         square_intensity(3, 0, 7)
         gate_group(2)
         quantize_h(2, GATES)
-        new = roots("roots_c", GATES + 2, 3)
+        new = roots("roots_c", GATES + 2, 4)
         replace(3, 0, 2, 1, new[0])
         replace(0, 2, 2, 2, new[1])
         replace(1, 2, 2, 3, new[2])
+        replace(2, 2, 2, 0, new[3])
         seasoning(2)
         square_intensity(0, 1, 6)
         square_intensity(1, 1, 7)
         gate_group(3)
         quantize_h(3, GATES + 2)
-        new = roots("roots_d", GATES + 4, 4)
-        replace(2, 2, 2, 0, new[0])
-        replace(3, 2, 2, 1, new[1])
-        replace(0, 4, 2, 6, new[2])
-        replace(1, 4, 2, 7, new[3])
-        seasoning(3)
         square_intensity(2, 1, 2)
+        new = roots("roots_d", GATES + 4, 4)
+        replace(3, 2, 2, 1, new[0])
+        replace(0, 4, 2, 6, new[1])
+        replace(1, 4, 2, 7, new[2])
+        replace(2, 4, 2, 2, new[3])
+        seasoning(3)
         square_intensity(3, 1, 3)
-        new = roots("roots_e", PLAIN, 2)
-        for nt in range(2):
-            replace(nt, 6, 2, nt, new[nt])
+        new = roots("roots_e", PLAIN, 3)
+        for nt in range(3):
+            replace(nt, 6, 2, (0, 1, 6)[nt], new[nt])
             store(nt)
-        for nt in range(2, 4):
-            last = placed(f"root_last{nt}", PLAIN + 2 * nt, [P, 2 * GR], F32)
-            replace(nt, 4, 4, nt, last[:])
-            store(nt)
+        last = placed("root_last", PLAIN + 4, [P, 2 * GR], F32)
+        replace(3, 4, 4, 3, last[:])
+        store(3)

@@ -25,10 +25,10 @@ GR = 2 * CH
 KIB = 1024
 
 SLOT_A, IDENT, SLOT_B, SLOT_C = 0, 8.5, 9, 17
-ROUNDED = (25, 29, 33, 38)
-WO_SCALES, WO_WORDS, H_ROWS, PAGE3 = 33, 33.5, 37.5, 41.5
+ROUNDED = (25.5, 72, 33.5, 38.5)
+WO_SCALES, PAGE2, WO_WORDS, H_ROWS, PAGE3 = SLOT_C, SLOT_C + 0.5, 33.5, 38.5, 172
 GATES, PLAIN, Y_SQ, G_SQ, PICK1 = 50, 82, 114, 130, 148
-FIRST_ROOT = 160
+FIRST_ROOT = 166
 
 
 def tile_list_sauce_seasoning_kernel(
@@ -166,16 +166,20 @@ def tile_list_sauce_seasoning_kernel(
         quantize_w1(1, 0)
         wo = placed("wo", WO_WORDS, [P, 2, N], I32)
         nc.sync.dma_start(wo[:], wo_words.rearrange("a p c i -> p a (c i)").bitcast(I32))
+        round_w1(1, 1)
+        load_page(2, PAGE2)
         wo_sc = placed("wo_sc", WO_SCALES, [P, N], U8)
-        nc.vector.memset(wo_sc[:].bitcast(I32), 0)
+        more_zeros = placed("more_zeros", PAGE3, [P, 32], I32)
+        nc.gpsimd.memset(more_zeros[:], 0)
+        nc.vector.tensor_copy(
+            wo_sc[:].bitcast(I32).rearrange("p (r w) -> p r w", w=32), more_zeros[:].unsqueeze(1).to_broadcast([P, 4, 32])
+        )
         for q in range(4):
             nc.sync.dma_start(
                 wo_sc[32 * q : 32 * q + 8, :].bitcast(I32), wo_scales[:, 4 * q : 4 * q + 4, :].bitcast(I32)
             )
-        round_w1(1, 1)
-        load_page(2, SLOT_C)
-        quantize_w1(1, 1)
         load_page(3, PAGE3)
+        quantize_w1(1, 1)
 
         logits, gate, plain, hq, h_rows = {}, {}, {}, {}, {}
 
@@ -270,14 +274,14 @@ def tile_list_sauce_seasoning_kernel(
             gate_features(g, 0)
             gate_features(g, 1)
 
-        y_sq, g_pick, g_sq = {}, {}, {}
+        y_sq, y_bank, g_pick, g_sq = {}, {}, {}, {}
 
         def quantize_h(g, kib=None):
             made = quantize(f"hq{g}", h_rows[g][:].rearrange("p r j u e -> p (r j u e)"), 2 * GR, kib)
             for i, operand in enumerate(made):
                 hq[i // 2, 2 * g + i % 2] = operand
 
-        def seasoning(g):
+        def seasoning(g, pages=4):
             for c in (2 * g, 2 * g + 1):
                 bank = bank_tile(f"y{c}", 4 + c % 2, [P, N])
                 for rb in range(2):
@@ -291,9 +295,16 @@ def tile_list_sauce_seasoning_kernel(
                         start=(rb == 0),
                         stop=(rb == 1),
                     )
-                sq = placed(f"y_sq{c}", Y_SQ + 2 * c, [P, N], F32)
-                nc.scalar.activation(sq[:], bank[:], ACT.Square)
-                y_sq[c] = sq
+                y_bank[c] = bank
+                square_seasoning(c, 0, pages)
+
+        def square_seasoning(c, first, count):
+            sq = placed(f"y_sq{c}{first}", Y_SQ + 2 * c, [P, count, P], F32)
+            nc.scalar.activation(
+                sq[:].rearrange("p n m -> p (n m)"), y_bank[c][:, first * P : (first + count) * P], ACT.Square
+            )
+            for i in range(count):
+                y_sq[c, first + i] = sq[:, i, :]
 
         def pick_intensity(nt, kib):
             picked = placed(f"g_pick{nt}", kib, [P, S], F32)
@@ -323,7 +334,7 @@ def tile_list_sauce_seasoning_kernel(
             for i in range(count):
                 nc.tensor.matmul(
                     bank[:, i, :],
-                    y_sq[first + i][:, nt * P : (nt + 1) * P],
+                    y_sq[first + i, nt],
                     ident[:],
                     start=False,
                     stop=(i == count - 1),
@@ -341,65 +352,70 @@ def tile_list_sauce_seasoning_kernel(
         for g, rb, u in first_half:
             gate_pass(g, rb, u, 1)
             sigmoid(g, rb, u)
-        features(0, 0, (6, 7))
         gates(2, 0)
+        features(0, 0, (0, 1))
+        gates(3, 1)
         gates(3, 0)
         gates(2, 1)
-        gates(3, 1)
-        direct = [chunk_features(1, c, c) for c in range(2)]
-        features(1, 0, (2, 3))
+        direct = [chunk_features(1, c, 6 + c) for c in range(2)]
+        features(1, 1, (0, 1))
         root_warm = kept("root_warm", [P, 1], F32)
-        nc.scalar.activation(root_warm[:], gate[3, 1][:, 1, 0, 0:1], ACT.Sqrt)
+        nc.scalar.activation(root_warm[:], plain[1, 1][:, 1, 0, 0:1], ACT.Sqrt, scale=0.0, bias=gate[2, 1][:, 1, 0, 0:1])
         pick_intensity(0, ROUNDED[0])
         open_h(0)
         gate_features(0, 0)
         for c in range(2):
             gate_chunk(1, c, direct[c])
-        features(1, 1, (0, 1))
+        features(1, 0, (0, 1))
         quantize_h(0)
         square_intensity(0, 0, 6)
-        seasoning(0)
+        seasoning(0, pages=1)
         pick_intensity(1, PICK1)
         pick_intensity(2, PICK1 + 4)
         new = roots("roots_a", FIRST_ROOT, 1)
         replace(0, 0, 2, 6, new[0])
-        gate_group(1)
+        for c in range(2):
+            square_seasoning(c, 1, 3)
+        open_h(1)
+        gate_features(1, 1)
+        gate_features(1, 0)
         features(2, 0, (4, 5))
         square_intensity(1, 0, 6)
         features(2, 1, (4, 5))
         quantize_h(1, FIRST_ROOT - 1.5)
         pick_intensity(3, FIRST_ROOT + 0.5)
-        new = roots("roots_b", GATES + 1, 2)
+        new = roots("roots_b", GATES + 1, 3)
         replace(1, 0, 2, 7, new[0])
         square_intensity(2, 0, 6)
         replace(2, 0, 2, 0, new[1])
         seasoning(1)
+        square_intensity(3, 0, 4)
+        replace(3, 0, 2, 1, new[2])
         features(3, 0, (4, 5))
         features(3, 1, (4, 5))
-        square_intensity(3, 0, 7)
         gate_group(2)
         quantize_h(2, GATES)
         new = roots("roots_c", GATES + 2, 4)
-        replace(3, 0, 2, 1, new[0])
-        replace(0, 2, 2, 2, new[1])
-        replace(1, 2, 2, 3, new[2])
-        replace(2, 2, 2, 0, new[3])
+        for nt in range(4):
+            replace(nt, 2, 2, (2, 3, 0, 1)[nt], new[nt])
         seasoning(2)
         square_intensity(0, 1, 6)
         square_intensity(1, 1, 7)
         gate_group(3)
         quantize_h(3, GATES + 2)
         square_intensity(2, 1, 2)
-        new = roots("roots_d", GATES + 4, 4)
-        replace(3, 2, 2, 1, new[0])
-        replace(0, 4, 2, 6, new[1])
-        replace(1, 4, 2, 7, new[2])
-        replace(2, 4, 2, 2, new[3])
-        seasoning(3)
-        square_intensity(3, 1, 3)
-        new = roots("roots_e", PLAIN, 3)
+        new = roots("roots_d", GATES + 4, 3)
         for nt in range(3):
-            replace(nt, 6, 2, (0, 1, 6)[nt], new[nt])
+            replace(nt, 4, 2, (6, 7, 2)[nt], new[nt])
+        square_intensity(3, 1, 3)
+        seasoning(3, pages=1)
+        new = roots("roots_e", PLAIN, 3)
+        replace(0, 6, 2, 0, new[0])
+        store(0)
+        for c in range(6, 8):
+            square_seasoning(c, 1, 3)
+        for nt in range(1, 3):
+            replace(nt, 6, 2, (1, 6)[nt - 1], new[nt])
             store(nt)
         last = placed("root_last", PLAIN + 4, [P, 2 * GR], F32)
         replace(3, 4, 4, 3, last[:])

@@ -128,9 +128,11 @@ def tile_list_sauce_seasoning_kernel(
         load_w1(0, 0, SLOT_C)
         v = {}
         for a in range(2):
-            for hf in range(2):
-                v[a, hf] = kept(f"v{a}{hf}", [P, S // 2], U32)
-                nc.vector.tensor_copy(v[a, hf][:], tab[a][:].bitcast(U32).indirect(listed(4 * hf, 4)))
+            for first, count in ((0, 2), (2, 2), (4, 4)):
+                words = kept(f"v{a}{first}", [P, count * CH], U32)
+                nc.vector.tensor_copy(words[:], tab[a][:].bitcast(U32).indirect(listed(first, count)))
+                for i in range(count // 2):
+                    v[a, first // 2 + i] = words[:, i * GR : (i + 1) * GR]
             load_w1(a, 1 - a, (SLOT_A, SLOT_B)[a])
 
         def quantize(name, src, width, kib=None):
@@ -184,9 +186,9 @@ def tile_list_sauce_seasoning_kernel(
         logits, gate, plain, hq, h_rows = {}, {}, {}, {}, {}
 
         def moving(a, first, width):
-            col = first % (S // 2)
+            col = first % GR
             return {
-                "rhs": v[a, first // (S // 2)][:, col : col + width].bitcast(FP8X4),
+                "rhs": v[a, first // GR][:, col : col + width].bitcast(FP8X4),
                 "rhs_scale": v_planes[a][:, first : first + width],
             }
 
@@ -346,7 +348,7 @@ def tile_list_sauce_seasoning_kernel(
         def store(nt):
             nc.sync.dma_start(out[nt * P : (nt + 1) * P, :], page[nt][:])
 
-        first_half = [(g, rb, u) for rb in range(2) for g in range(2) for u in range(2)]
+        first_half = [(g, rb, u) for g in range(2) for rb in range(2) for u in range(2)]
         for g, rb, u in first_half:
             gate_pass(g, rb, u, 0)
         for g, rb, u in first_half:

@@ -26,9 +26,9 @@ KIB = 1024
 
 SLOT_A, IDENT, SLOT_B, SLOT_C = 0, 8.5, 9, 17
 ROUNDED = (25.5, 72, 33.5, 38.5)
-WO_SCALES, PAGE2, WO_WORDS, H_ROWS, PAGE3 = SLOT_C, SLOT_C + 0.5, 33.5, 38.5, 172
-GATES, PLAIN, Y_SQ, G_SQ, PICK1 = 50, 82, 114, 130, 148
-FIRST_ROOT = 166
+WO_SCALES, PAGE2, H_ROWS, WO_WORDS, PAGE3 = SLOT_C, SLOT_C + 0.5, 34, 42, 184
+GATES, PLAIN, Y_SQ, G_SQ, PICKS = 50, 82, 114, 130, 146
+QUARTER3 = 172
 
 
 def tile_list_sauce_seasoning_kernel(
@@ -135,12 +135,15 @@ def tile_list_sauce_seasoning_kernel(
                     v[a, first // 2 + i] = words[:, i * GR : (i + 1) * GR]
             load_w1(a, 1 - a, (SLOT_A, SLOT_B)[a])
 
-        def quantize(name, src, width, kib=None):
+        def quantize(name, src, width, kib=None, plane_kib=None):
             if kib is None:
                 codes = kept(f"{name}_codes", [P, width], U32)
             else:
                 codes = placed(f"{name}_codes", kib, [P, width], U32)
-            scales = kept(f"{name}_scales", [P, width], U8)
+            if plane_kib is None:
+                scales = kept(f"{name}_scales", [P, width], U8)
+            else:
+                scales = placed(f"{name}_scales", plane_kib, [P, width], U8)
             nc.vector.quantize_mx(out=codes[:].bitcast(FP8X4), scales=scales[:], in_=src)
             return [(codes[:, i : i + P], scales[:, i : i + P]) for i in range(0, width, P)]
 
@@ -166,24 +169,18 @@ def tile_list_sauce_seasoning_kernel(
         round_w1(1, 0)
         load_page(1, SLOT_B)
         quantize_w1(1, 0)
-        wo = placed("wo", WO_WORDS, [P, 2, N], I32)
-        nc.sync.dma_start(wo[:], wo_words.rearrange("a p c i -> p a (c i)").bitcast(I32))
         round_w1(1, 1)
         load_page(2, PAGE2)
         wo_sc = placed("wo_sc", WO_SCALES, [P, N], U8)
-        more_zeros = placed("more_zeros", PAGE3, [P, 32], I32)
-        nc.gpsimd.memset(more_zeros[:], 0)
-        nc.vector.tensor_copy(
-            wo_sc[:].bitcast(I32).rearrange("p (r w) -> p r w", w=32), more_zeros[:].unsqueeze(1).to_broadcast([P, 4, 32])
-        )
         for q in range(4):
             nc.sync.dma_start(
                 wo_sc[32 * q : 32 * q + 8, :].bitcast(I32), wo_scales[:, 4 * q : 4 * q + 4, :].bitcast(I32)
             )
-        load_page(3, PAGE3)
         quantize_w1(1, 1)
+        wo = placed("wo", WO_WORDS, [P, 2, N], I32)
+        nc.sync.dma_start(wo[:], wo_words.rearrange("a p c i -> p a (c i)").bitcast(I32))
 
-        logits, gate, plain, hq, h_rows = {}, {}, {}, {}, {}
+        logits, gate, chunk_gate, plain, hq, h_rows = {}, {}, {}, {}, {}, {}
 
         def moving(a, first, width):
             col = first % GR
@@ -191,12 +188,6 @@ def tile_list_sauce_seasoning_kernel(
                 "rhs": v[a, first // GR][:, col : col + width].bitcast(FP8X4),
                 "rhs_scale": v_planes[a][:, first : first + width],
             }
-
-        def gate_place(g, rb):
-            return PICK1 - 2 + 4 * rb if g == 0 else GATES + 4 * (2 * g + rb)
-
-        def plain_place(g, rb):
-            return PICK1 + 6 if g == 0 else PLAIN + 4 * (2 * g + rb)
 
         def gate_pass(g, rb, u, a):
             if a == 0:
@@ -214,9 +205,16 @@ def tile_list_sauce_seasoning_kernel(
                 )
 
         def sigmoid(g, rb, u):
-            if u == 0:
-                gate[g, rb] = placed(f"gate{g}{rb}", gate_place(g, rb), [P, 2, GR, 2], F32)
-            nc.scalar.activation(gate[g, rb][:, u], logits[g, rb, u][:].rearrange("p e j -> p j e"), ACT.Sigmoid)
+            pairs = logits[g, rb, u][:].rearrange("p e j -> p j e")
+            if (g, rb) == (0, 1):
+                for c in range(2):
+                    if u == 0:
+                        chunk_gate[c] = placed(f"gate_chunk{c}", (PICKS + 5.5, GATES + 4)[c], [P, 2, CH, 2], F32)
+                    nc.scalar.activation(chunk_gate[c][:, u], pairs[:, c * CH : (c + 1) * CH, :], ACT.Sigmoid)
+            else:
+                if u == 0:
+                    gate[g, rb] = placed(f"gate{g}{rb}", GATES + 4 * (2 * g + rb), [P, 2, GR, 2], F32)
+                nc.scalar.activation(gate[g, rb][:, u], pairs, ACT.Sigmoid)
 
         def gates(g, rb):
             for u in range(2):
@@ -237,7 +235,7 @@ def tile_list_sauce_seasoning_kernel(
                 )
 
         def features(g, rb, banks):
-            copied = placed(f"a_plain{g}{rb}", plain_place(g, rb), [P, 2, GR, 2], F32)
+            copied = placed(f"a_plain{g}{rb}", PAGE3 + 4 if g == 0 else PLAIN + 4 * (2 * g + rb), [P, 2, GR, 2], F32)
             for u in range(2):
                 bank = bank_tile(f"a{g}{rb}{u}", banks[u], [P, 2, GR])
                 for e in range(2):
@@ -251,23 +249,29 @@ def tile_list_sauce_seasoning_kernel(
                 feature_passes(bank[:, t, :], rb, t, c * CH, CH)
             return bank
 
-        def open_h(g):
-            h_rows[g] = placed(f"h_bf{g}", H_ROWS, [P, 2, GR, 2, 2], BF16)
+        h_space = placed("h_bf", H_ROWS, [P, 5 * KP], BF16)
 
-        def gate_features(g, rb):
+        def open_h(g):
+            start = KP if g == 0 else 0
+            h_rows[g] = h_space[:, start : start + 4 * KP].rearrange("p (r j u e) -> p r j u e", r=2, u=2, e=2)
+
+        def block_place(g, rb):
+            return 1 - rb if g == 1 else rb
+
+        def gate_features(g, rb, first=0, count=2):
+            cols = slice(first * CH, (first + count) * CH)
             nc.gpsimd.tensor_tensor(
-                h_rows[g][:, rb],
-                plain[g, rb][:].rearrange("p u j e -> p j u e"),
-                gate[g, rb][:].rearrange("p u j e -> p j u e"),
+                h_rows[g][:, block_place(g, rb), cols],
+                plain[g, rb][:, :, cols, :].rearrange("p u j e -> p j u e"),
+                gate[g, rb][:, :, cols, :].rearrange("p u j e -> p j u e"),
                 ALU.mult,
             )
 
-        def gate_chunk(rb, c, bank):
-            cols = slice(c % 2 * CH, (c % 2 + 1) * CH)
-            nc.vector.tensor_tensor(
-                h_rows[c // 2][:, rb, cols],
-                bank[:].rearrange("p (u e) j -> p j u e", e=2),
-                gate[c // 2, rb][:, :, cols, :].rearrange("p u j e -> p j u e"),
+        def gate_chunk(engine, c, sums):
+            engine.tensor_tensor(
+                h_rows[0][:, 1, c * CH : (c + 1) * CH],
+                sums,
+                chunk_gate[c][:].rearrange("p u j e -> p j u e"),
                 ALU.mult,
             )
 
@@ -276,74 +280,78 @@ def tile_list_sauce_seasoning_kernel(
             gate_features(g, 0)
             gate_features(g, 1)
 
-        y_sq, y_bank, g_pick, g_sq = {}, {}, {}, {}
+        y_sq, g_pick, g_sq = {}, {}, {}
 
-        def quantize_h(g, kib=None):
-            made = quantize(f"hq{g}", h_rows[g][:].rearrange("p r j u e -> p (r j u e)"), 2 * GR, kib)
+        def quantize_h(g, kib=None, plane_kib=None):
+            made = quantize(f"hq{g}", h_rows[g].rearrange("p r j u e -> p (r j u e)"), 2 * GR, kib, plane_kib)
             for i, operand in enumerate(made):
-                hq[i // 2, 2 * g + i % 2] = operand
+                hq[block_place(g, i // 2), 2 * g + i % 2] = operand
 
-        def seasoning(g, pages=4):
-            for c in (2 * g, 2 * g + 1):
-                bank = bank_tile(f"y{c}", 4 + c % 2, [P, N])
+        def seasoning(g, first, count, b):
+            cols = slice(first * P, (first + count) * P)
+            bank = bank_tile(f"y{g}{first}", b, [P, 2, count * P])
+            for i in range(2):
                 for rb in range(2):
-                    codes, scales = hq[rb, c]
+                    codes, scales = hq[rb, 2 * g + i]
                     nc.tensor.matmul_mx(
-                        out=bank[:],
+                        out=bank[:, i, :],
                         lhsT=codes.bitcast(FP8X4),
                         lhsT_scale=scales,
-                        rhs=wo[:, rb, :].bitcast(FP8X4),
-                        rhs_scale=wo_sc[4 * rb : P, :],
+                        rhs=wo[:, rb, cols].bitcast(FP8X4),
+                        rhs_scale=wo_sc[4 * rb : P, cols],
                         start=(rb == 0),
                         stop=(rb == 1),
                     )
-                y_bank[c] = bank
-                square_seasoning(c, 0, pages)
+            for k in range(count):
+                nt = first + k
+                sq = placed(f"y_sq{g}{nt}", Y_SQ + 4 * g + nt, [P, 2, P], F32)
+                nc.scalar.activation(sq[:], bank[:, :, k * P : (k + 1) * P], ACT.Square)
+                for i in range(2):
+                    y_sq[2 * g + i, nt] = sq[:, i, :]
 
-        def square_seasoning(c, first, count):
-            sq = placed(f"y_sq{c}{first}", Y_SQ + 2 * c, [P, count, P], F32)
-            nc.scalar.activation(
-                sq[:].rearrange("p n m -> p (n m)"), y_bank[c][:, first * P : (first + count) * P], ACT.Square
-            )
+        def pick_intensity(nt, first=0, count=8, kib=None):
+            place = PICKS + 4 * nt + first / 2 if kib is None else kib
+            picked = placed(f"g_pick{nt}{first}", place, [P, count * CH], F32)
+            nc.vector.tensor_copy(picked[:], page[nt][:].indirect(listed(first, count)))
             for i in range(count):
-                y_sq[c, first + i] = sq[:, i, :]
+                g_pick[nt, first + i] = picked[:, i * CH : (i + 1) * CH]
 
-        def pick_intensity(nt, kib):
-            picked = placed(f"g_pick{nt}", kib, [P, S], F32)
-            nc.vector.tensor_copy(picked[:], page[nt][:].indirect(offsets[:]))
-            g_pick[nt] = picked
+        def turn_pick(nt, first, count, b):
+            bank = bank_tile(f"g{nt}{first}", b, [P, count, P])
+            for i in range(count):
+                nc.tensor.transpose(bank[:, i, :], g_pick[nt, first + i], ident[:])
+            return nt, first, count, bank
 
-        def square_intensity(nt, hf, b):
-            bank = bank_tile(f"g{nt}{hf}", b, [P, 4, P])
-            for i in range(4):
-                c = 4 * hf + i
-                nc.tensor.transpose(bank[:, i, :], g_pick[nt][:, c * CH : (c + 1) * CH], ident[:])
-            sq = placed(f"g_sq{nt}{hf}", G_SQ + 2 * (2 * nt + hf), [P, 4, P], F32)
+        def square_pick(nt, first, count, bank):
+            sq = placed(f"g_sq{nt}{first}", G_SQ + 4 * nt + first / 2, [P, count, P], F32)
             nc.scalar.activation(sq[:], bank[:], ACT.Square)
-            g_sq[nt, hf] = sq
+            for i in range(count):
+                g_sq[nt, first + i] = sq[:, i, :]
+
+        def square_intensity(nt, first, count, b):
+            square_pick(*turn_pick(nt, first, count, b))
 
         def roots(name, kib, count):
             rows = placed(name, kib, [P, count, GR], F32)
             return [rows[:, i, :] for i in range(count)]
 
-        def replace(nt, first, count, b, new):
+        def open_sum(nt, first, count, b):
             bank = bank_tile(f"sum{nt}{first}", b, [P, count, CH])
-            for i in range(count):
-                c = first + i
+            picked = [g_sq[nt, c] for c in range(first, first + count)]
+            made = [y_sq[c, nt] for c in range(first, first + count)]
+            terms = picked + made if nt + first == 0 else made + picked
+            for i, term in enumerate(terms):
                 nc.tensor.matmul(
-                    bank[:, i, :], g_sq[nt, c // 4][:, c % 4, :], ident[:], start=(i == 0), stop=False, is_transpose=True
+                    bank[:, i % count, :], term, ident[:], start=(i == 0), stop=(i == 2 * count - 1), is_transpose=True
                 )
-            for i in range(count):
-                nc.tensor.matmul(
-                    bank[:, i, :],
-                    y_sq[first + i, nt],
-                    ident[:],
-                    start=False,
-                    stop=(i == count - 1),
-                    is_transpose=True,
-                )
+            return nt, first, count, bank
+
+        def scatter_root(nt, first, count, bank, new):
             nc.scalar.activation(new, bank[:].rearrange("p i j -> p (i j)"), ACT.Sqrt)
             nc.vector.tensor_copy(page[nt][:].indirect(listed(first, count)), new)
+
+        def replace(nt, first, count, b, new):
+            scatter_root(*open_sum(nt, first, count, b), new)
 
         def store(nt):
             nc.sync.dma_start(out[nt * P : (nt + 1) * P, :], page[nt][:])
@@ -360,65 +368,69 @@ def tile_list_sauce_seasoning_kernel(
         gates(3, 0)
         gates(2, 1)
         direct = [chunk_features(1, c, 6 + c) for c in range(2)]
+        chunk_plain = placed("a_chunk", PLAIN, [P, CH, 2, 2], F32)
+        nc.scalar.copy(chunk_plain[:], direct[1][:].rearrange("p (u e) j -> p j u e", e=2))
         features(1, 1, (0, 1))
         root_warm = kept("root_warm", [P, 1], F32)
         nc.scalar.activation(root_warm[:], plain[1, 1][:, 1, 0, 0:1], ACT.Sqrt, scale=0.0, bias=gate[2, 1][:, 1, 0, 0:1])
-        pick_intensity(0, ROUNDED[0])
+        pick_intensity(0)
         open_h(0)
         gate_features(0, 0)
-        for c in range(2):
-            gate_chunk(1, c, direct[c])
-        features(1, 0, (0, 1))
-        quantize_h(0)
-        square_intensity(0, 0, 6)
-        seasoning(0, pages=1)
-        pick_intensity(1, PICK1)
-        pick_intensity(2, PICK1 + 4)
-        new = roots("roots_a", FIRST_ROOT, 1)
-        replace(0, 0, 2, 6, new[0])
-        for c in range(2):
-            square_seasoning(c, 1, 3)
+        load_page(3, PAGE3)
+        gate_chunk(nc.vector, 0, direct[0][:].rearrange("p (u e) j -> p j u e", e=2))
+        gate_chunk(nc.gpsimd, 1, chunk_plain[:])
         open_h(1)
-        gate_features(1, 1)
+        gate_features(1, 1, 0, 1)
+        features(1, 0, (0, 1))
+        square_intensity(0, 0, 4, 6)
+        pick_intensity(1, 0, 4, PICKS + 4.5)
+        pick_intensity(1, 4, 4, PICKS + 6.5)
+        square_intensity(1, 0, 4, 7)
+        quantize_h(0, plane_kib=PICKS + 4.25)
+        gate_features(1, 1, 1, 1)
         gate_features(1, 0)
-        features(2, 0, (4, 5))
-        square_intensity(1, 0, 6)
-        features(2, 1, (4, 5))
-        quantize_h(1, FIRST_ROOT - 1.5)
-        pick_intensity(3, FIRST_ROOT + 0.5)
-        new = roots("roots_b", GATES + 1, 3)
-        replace(1, 0, 2, 7, new[0])
-        square_intensity(2, 0, 6)
-        replace(2, 0, 2, 0, new[1])
-        seasoning(1)
-        square_intensity(3, 0, 4)
-        replace(3, 0, 2, 1, new[2])
-        features(3, 0, (4, 5))
-        features(3, 1, (4, 5))
+        features(2, 0, (0, 1))
+        pick_intensity(2, kib=PICKS + 9)
+        seasoning(0, 0, 2, 4)
+        seasoning(0, 2, 2, 5)
+        square_intensity(2, 0, 4, 4)
+        pick_intensity(3, 0, 2, QUARTER3)
+        pick_intensity(3, 2, 6, PICKS + 13)
+        late_pick = turn_pick(3, 0, 2, 1)
+        quantize_h(1, plane_kib=QUARTER3 + 0.25)
+        new = roots("roots_a", QUARTER3 - 2.75, 3)
+        replace(0, 0, 2, 6, new[0])
+        square_pick(*late_pick)
+        replace(1, 0, 2, 1, new[1])
+        features(2, 1, (6, 1))
+        replace(2, 0, 2, 6, new[2])
+        replace(3, 0, 2, 1, roots("root_b", QUARTER3 + 0.75, 1)[0])
         gate_group(2)
-        quantize_h(2, GATES)
-        new = roots("roots_c", GATES + 2, 4)
-        for nt in range(4):
-            replace(nt, 2, 2, (2, 3, 0, 1)[nt], new[nt])
-        seasoning(2)
-        square_intensity(0, 1, 6)
-        square_intensity(1, 1, 7)
-        gate_group(3)
-        quantize_h(3, GATES + 2)
-        square_intensity(2, 1, 2)
-        new = roots("roots_d", GATES + 4, 3)
+        seasoning(1, 0, 2, 6)
+        seasoning(1, 2, 2, 1)
+        square_intensity(3, 2, 2, 6)
+        features(3, 0, (6, 1))
+        quantize_h(2, plane_kib=QUARTER3 + 1.5)
+        new = roots("roots_c", QUARTER3 - 5.5, 3)
         for nt in range(3):
-            replace(nt, 4, 2, (6, 7, 2)[nt], new[nt])
-        square_intensity(3, 1, 3)
-        seasoning(3, pages=1)
-        new = roots("roots_e", PLAIN, 3)
-        replace(0, 6, 2, 0, new[0])
-        store(0)
-        for c in range(6, 8):
-            square_seasoning(c, 1, 3)
-        for nt in range(1, 3):
-            replace(nt, 6, 2, (1, 6)[nt - 1], new[nt])
+            replace(nt, 2, 2, 2 + nt, new[nt])
+        replace(3, 2, 2, 5, roots("root_d", QUARTER3, 1)[0])
+        features(3, 1, (2, 3))
+        gate_group(3)
+        for nt in range(4):
+            square_intensity(nt, 4, 4, (4, 5, 2, 3)[nt])
+        seasoning(2, 0, 2, 4)
+        seasoning(2, 2, 2, 5)
+        quantize_h(3, plane_kib=QUARTER3 + 0.75)
+        new = roots("roots_e", QUARTER3 - 8.25, 3)
+        for nt in range(3):
+            replace(nt, 4, 2, (0, 1, 7)[nt], new[nt])
+        seasoning(3, 0, 2, 0)
+        seasoning(3, 2, 2, 1)
+        new = roots("roots_f", QUARTER3 + 3, 3)
+        for nt in range(3):
+            replace(nt, 6, 2, 3 + nt, new[nt])
             store(nt)
-        last = placed("root_last", PLAIN + 4, [P, 2 * GR], F32)
-        replace(3, 4, 4, 3, last[:])
+        last = placed("root_last", QUARTER3 + 6, [P, 2 * GR], F32)
+        replace(3, 4, 4, 6, last[:])
         store(3)

@@ -177,8 +177,16 @@ def tile_list_sauce_seasoning_kernel(
                 wo_sc[32 * q : 32 * q + 8, :].bitcast(I32), wo_scales[:, 4 * q : 4 * q + 4, :].bitcast(I32)
             )
         quantize_w1(1, 1)
-        wo = placed("wo", WO_WORDS, [P, 2, N], I32)
-        nc.sync.dma_start(wo[:], wo_words.rearrange("a p c i -> p a (c i)").bitcast(I32))
+        wo = {}
+
+        def load_wo(pair, kib):
+            words = placed(f"wo{pair}", kib, [P, 2, GR], I32)
+            nc.sync.dma_start(
+                words[:], wo_words[:, :, pair * GR : (pair + 1) * GR, :].rearrange("a p c i -> p a (c i)").bitcast(I32)
+            )
+            wo[pair] = words
+
+        load_wo(0, WO_WORDS)
 
         logits, gate, chunk_gate, plain, hq, h_rows = {}, {}, {}, {}, {}, {}
 
@@ -235,7 +243,7 @@ def tile_list_sauce_seasoning_kernel(
                 )
 
         def features(g, rb, banks):
-            copied = placed(f"a_plain{g}{rb}", PAGE3 + 4 if g == 0 else PLAIN + 4 * (2 * g + rb), [P, 2, GR, 2], F32)
+            copied = placed(f"a_plain{g}{rb}", PAGE3 + 6 if g == 0 else PLAIN + 4 * (2 * g + rb), [P, 2, GR, 2], F32)
             for u in range(2):
                 bank = bank_tile(f"a{g}{rb}{u}", banks[u], [P, 2, GR])
                 for e in range(2):
@@ -297,7 +305,7 @@ def tile_list_sauce_seasoning_kernel(
                         out=bank[:, i, :],
                         lhsT=codes.bitcast(FP8X4),
                         lhsT_scale=scales,
-                        rhs=wo[:, rb, cols].bitcast(FP8X4),
+                        rhs=wo[first // 2][:, rb, :].bitcast(FP8X4),
                         rhs_scale=wo_sc[4 * rb : P, cols],
                         start=(rb == 0),
                         stop=(rb == 1),
@@ -377,6 +385,7 @@ def tile_list_sauce_seasoning_kernel(
         open_h(0)
         gate_features(0, 0)
         load_page(3, PAGE3)
+        load_wo(1, PAGE3 + 8)
         gate_chunk(nc.vector, 0, direct[0][:].rearrange("p (u e) j -> p j u e", e=2))
         gate_chunk(nc.gpsimd, 1, chunk_plain[:])
         open_h(1)
@@ -402,34 +411,37 @@ def tile_list_sauce_seasoning_kernel(
         replace(0, 0, 2, 6, new[0])
         square_pick(*late_pick)
         replace(1, 0, 2, 1, new[1])
-        features(2, 1, (6, 1))
-        replace(2, 0, 2, 6, new[2])
-        replace(3, 0, 2, 1, roots("root_b", QUARTER3 + 0.75, 1)[0])
+        replace(3, 0, 2, 0, new[2])
+        replace(2, 0, 2, 6, roots("root_b", QUARTER3 + 0.75, 1)[0])
+        features(2, 1, (1, 0))
         gate_group(2)
         seasoning(1, 0, 2, 6)
         seasoning(1, 2, 2, 1)
-        square_intensity(3, 2, 2, 6)
-        features(3, 0, (6, 1))
         quantize_h(2, plane_kib=QUARTER3 + 1.5)
         new = roots("roots_c", QUARTER3 - 5.5, 3)
-        for nt in range(3):
-            replace(nt, 2, 2, 2 + nt, new[nt])
+        replace(0, 2, 2, 2, new[0])
+        square_intensity(3, 2, 2, 0)
+        replace(1, 2, 2, 3, new[1])
+        features(3, 0, (6, 1))
+        replace(2, 2, 2, 4, new[2])
         replace(3, 2, 2, 5, roots("root_d", QUARTER3, 1)[0])
-        features(3, 1, (2, 3))
+        features(3, 1, (0, 6))
         gate_group(3)
-        for nt in range(4):
-            square_intensity(nt, 4, 4, (4, 5, 2, 3)[nt])
-        seasoning(2, 0, 2, 4)
-        seasoning(2, 2, 2, 5)
+        square_intensity(0, 4, 4, 1)
+        square_intensity(1, 4, 4, 0)
+        seasoning(2, 0, 2, 6)
+        square_intensity(2, 4, 4, 2)
+        seasoning(2, 2, 2, 1)
+        square_intensity(3, 4, 4, 3)
         quantize_h(3, plane_kib=QUARTER3 + 0.75)
         new = roots("roots_e", QUARTER3 - 8.25, 3)
         for nt in range(3):
-            replace(nt, 4, 2, (0, 1, 7)[nt], new[nt])
-        seasoning(3, 0, 2, 0)
-        seasoning(3, 2, 2, 1)
+            replace(nt, 4, 2, (4, 5, 7)[nt], new[nt])
+        seasoning(3, 0, 2, 4)
+        seasoning(3, 2, 2, 5)
         new = roots("roots_f", QUARTER3 + 3, 3)
         for nt in range(3):
-            replace(nt, 6, 2, 3 + nt, new[nt])
+            replace(nt, 6, 2, nt, new[nt])
             store(nt)
         last = placed("root_last", QUARTER3 + 6, [P, 2 * GR], F32)
         replace(3, 4, 4, 6, last[:])

@@ -28,7 +28,7 @@ SLOT_A, IDENT, SLOT_B, SLOT_C = 0, 8.5, 9, 17
 ROUNDED = (25.5, 72, 33.5, 38.5)
 WO_SCALES, PAGE2, H_ROWS, WO_WORDS, PAGE3 = SLOT_C, SLOT_C + 0.5, 34, 42, 184
 GATES, PLAIN, Y_SQ, G_SQ, PICKS = 50, 82, 114, 130, 146
-QUARTER3 = 172
+QUARTER3, TAB_SCALES = 172, 180
 
 
 def tile_list_sauce_seasoning_kernel(
@@ -55,24 +55,16 @@ def tile_list_sauce_seasoning_kernel(
         def listed(first, count):
             return offsets[:, first * (CH // 16) : (first + count) * (CH // 16)]
 
-        wg_raw = kept("wg_raw", [P, 2, 2 * H], U8)
-        nc.sync.dma_start(wg_raw[:].bitcast(I32), wg_words.rearrange("a p b -> p a b").bitcast(I32))
         wg_sc_raw = placed("wg_sc_raw", SLOT_B - 0.25, [P, KP], U8)
         nc.sync.dma_start(wg_sc_raw[0:64, :].bitcast(I32), wg_scales.rearrange("a g (b c) -> (g b) a c", b=2).bitcast(I32))
-        tab_sc = placed("tab_sc", SLOT_C, [P, T], U8)
-        nc.vector.memset(tab_sc[:].bitcast(I32), 0)
-        for q in range(4):
-            nc.sync.dma_start(
-                tab_sc[32 * q : 32 * q + 4, :].bitcast(I32), tab_scales[0, 4 * q : 4 * q + 4, :].bitcast(I32)
-            )
-        nc.sync.dma_start(tab_sc[8:24, :].bitcast(I32), tab_scales[1].bitcast(I32))
-        zeros = placed("zeros", SLOT_A, [P, 32], I32)
-        nc.gpsimd.memset(zeros[:], 0)
-        wg_sc = kept("wg_sc", [P, 2 * H], U8)
-        nc.vector.tensor_copy(
-            wg_sc[:].bitcast(I32).rearrange("p (r w) -> p r w", w=32), zeros[:].unsqueeze(1).to_broadcast([P, 16, 32])
-        )
+        tab_sc = placed("tab_sc", TAB_SCALES, [P, T], U8)
+        nc.sync.dma_start(tab_sc[0:32, :].bitcast(I32), tab_scales.rearrange("a g t -> g a t").bitcast(I32))
+        wg_raw = placed("wg_raw", SLOT_C, [P, 2, 2 * H], U8)
+        nc.sync.dma_start(wg_raw[:].bitcast(I32), wg_words.rearrange("a p b -> p a b").bitcast(I32))
         nc.vector.memset(wg_sc_raw[64:P, :].bitcast(I32), 0)
+        nc.vector.memset(tab_sc[32:64, :].bitcast(I32), 0)
+        nc.vector.memset(tab_sc[64:P, :].bitcast(I32), 0)
+        wg_sc = kept("wg_sc", [P, 2 * H], U8)
 
         tab, w1_raw, page = {}, {}, {}
 
@@ -95,8 +87,6 @@ def tile_list_sauce_seasoning_kernel(
             page[nt] = rows
 
         load_words(0, SLOT_A)
-        v_sc1 = kept("v_sc1", [P, S], U8)
-        nc.vector.memset(v_sc1[:].bitcast(I32), 0)
         table_warm = kept("table_warm", [P, 1], F32)
         nc.gpsimd.memset(table_warm[:], 0.0)
         nc.scalar.activation(table_warm[:], table_warm[:], ACT.Sigmoid)
@@ -111,20 +101,25 @@ def tile_list_sauce_seasoning_kernel(
         ident = placed("ident", IDENT, [P, P], F32)
         make_identity(nc, ident[:])
         wg = {}
-        for rb in range(2):
-            block = kept(f"wg{rb}", [P, 2 * 2 * KP], U8)
+
+        def order_wg(rb, first, count, block):
             nc.scalar.copy(
-                block[:].bitcast(U16).rearrange("p (a t m) -> p a t m", a=2, t=PACK),
-                wg_raw[:].bitcast(U16)[:, :, rb * KP : (rb + 1) * KP].rearrange("p a (m t) -> p a t m", t=PACK),
+                block[:].bitcast(U16).rearrange("p (a t m) -> p a t m", a=count, t=PACK),
+                wg_raw[:]
+                .bitcast(U16)[:, first : first + count, rb * KP : (rb + 1) * KP]
+                .rearrange("p a (m t) -> p a t m", t=PACK),
             )
-            wg[rb] = block
+            for i in range(count):
+                wg[rb, first + i] = block[:, i * 2 * KP : (i + 1) * 2 * KP]
+
+        order_wg(0, 0, 2, kept("wg0", [P, 2 * 2 * KP], U8))
+        order_wg(1, 0, 1, kept("wg10", [P, 2 * KP], U8))
         v_sc_picked = kept("v_sc_picked", [P, S], U8)
         nc.vector.tensor_copy(v_sc_picked[:], tab_sc[:].indirect(offsets[:]))
+        v_sc = kept("v_sc", [P, 2 * S], U8)
         for q in range(4):
-            nc.sync.dma_start(
-                v_sc1[32 * q : 32 * q + 4, :].bitcast(I32), v_sc_picked[8 + 4 * q : 12 + 4 * q, :].bitcast(I32)
-            )
-        v_planes = (v_sc_picked, v_sc1)
+            nc.sync.dma_start(v_sc[32 * q : 32 * q + 4, :].bitcast(I32), v_sc_picked[8 * q : 8 * q + 8, :].bitcast(I32))
+        order_wg(1, 1, 1, placed("wg11", TAB_SCALES, [P, 2 * KP], U8))
         load_w1(0, 0, SLOT_C)
         v = {}
         for a in range(2):
@@ -194,21 +189,21 @@ def tile_list_sauce_seasoning_kernel(
             col = first % GR
             return {
                 "rhs": v[a, first // GR][:, col : col + width].bitcast(FP8X4),
-                "rhs_scale": v_planes[a][:, first : first + width],
+                "rhs_scale": v_sc[:, a * S + first : a * S + first + width],
             }
 
-        def gate_pass(g, rb, u, a):
-            if a == 0:
+        def gate_pass(g, rb, u, a, opens):
+            if opens:
                 logits[g, rb, u] = bank_tile(f"b{g}{rb}{u}", 4 * rb + 2 * (g % 2) + u, [P, 2, GR])
             for e in range(2):
                 t = 2 * u + e
                 col = rb * H + a * KP + t * P
                 nc.tensor.matmul_mx(
                     out=logits[g, rb, u][:, e, :],
-                    lhsT=wg[rb][:, 2 * (a * KP + t * P) : 2 * (a * KP + (t + 1) * P)].bitcast(FP4X4),
+                    lhsT=wg[rb, a][:, 2 * t * P : 2 * (t + 1) * P].bitcast(FP4X4),
                     lhsT_scale=wg_sc[:, col : col + P],
-                    start=(a == 0 and e == 0),
-                    stop=(a == 1 and e == 1),
+                    start=(opens and e == 0),
+                    stop=(not opens and e == 1),
                     **moving(a, g * GR, GR),
                 )
 
@@ -226,8 +221,8 @@ def tile_list_sauce_seasoning_kernel(
 
         def gates(g, rb):
             for u in range(2):
-                gate_pass(g, rb, u, 0)
-                gate_pass(g, rb, u, 1)
+                gate_pass(g, rb, u, 1, True)
+                gate_pass(g, rb, u, 0, False)
                 sigmoid(g, rb, u)
 
         def feature_passes(dst, rb, t, first, width):
@@ -364,12 +359,14 @@ def tile_list_sauce_seasoning_kernel(
         def store(nt):
             nc.sync.dma_start(out[nt * P : (nt + 1) * P, :], page[nt][:])
 
-        first_half = [(g, rb, u) for g in range(2) for rb in range(2) for u in range(2)]
-        for g, rb, u in first_half:
-            gate_pass(g, rb, u, 0)
-        for g, rb, u in first_half:
-            gate_pass(g, rb, u, 1)
-            sigmoid(g, rb, u)
+        for u in range(2):
+            gate_pass(0, 0, u, 0, True)
+        for u in range(2):
+            gate_pass(0, 0, u, 1, False)
+            sigmoid(0, 0, u)
+        gates(0, 1)
+        gates(1, 0)
+        gates(1, 1)
         gates(2, 0)
         features(0, 0, (0, 1))
         gates(3, 1)

@@ -58,12 +58,12 @@ def tile_list_sauce_seasoning_kernel(
         wg_sc_raw = placed("wg_sc_raw", SLOT_B - 0.25, [P, KP], U8)
         nc.sync.dma_start(wg_sc_raw[0:64, :].bitcast(I32), wg_scales.rearrange("a g (b c) -> (g b) a c", b=2).bitcast(I32))
         tab_sc = placed("tab_sc", TAB_SCALES, [P, T], U8)
-        nc.sync.dma_start(tab_sc[0:32, :].bitcast(I32), tab_scales.rearrange("a g t -> g a t").bitcast(I32))
+        nc.sync.dma_start(tab_sc[64:96, :].bitcast(I32), tab_scales.rearrange("a g t -> g a t").bitcast(I32))
         wg_raw = placed("wg_raw", SLOT_C, [P, 2, 2 * H], U8)
         nc.sync.dma_start(wg_raw[:].bitcast(I32), wg_words.rearrange("a p b -> p a b").bitcast(I32))
         nc.vector.memset(wg_sc_raw[64:P, :].bitcast(I32), 0)
-        nc.vector.memset(tab_sc[32:64, :].bitcast(I32), 0)
-        nc.vector.memset(tab_sc[64:P, :].bitcast(I32), 0)
+        nc.vector.memset(tab_sc[0:64, :].bitcast(I32), 0)
+        nc.vector.memset(tab_sc[96:P, :].bitcast(I32), 0)
         wg_sc = kept("wg_sc", [P, 2 * H], U8)
 
         tab, w1_raw, page = {}, {}, {}
@@ -118,7 +118,7 @@ def tile_list_sauce_seasoning_kernel(
         nc.vector.tensor_copy(v_sc_picked[:], tab_sc[:].indirect(offsets[:]))
         v_sc = kept("v_sc", [P, 2 * S], U8)
         for q in range(4):
-            nc.sync.dma_start(v_sc[32 * q : 32 * q + 4, :].bitcast(I32), v_sc_picked[8 * q : 8 * q + 8, :].bitcast(I32))
+            nc.sync.dma_start(v_sc[32 * q : 32 * q + 4, :].bitcast(I32), v_sc_picked[64 + 8 * q : 72 + 8 * q, :].bitcast(I32))
         order_wg(1, 1, 1, placed("wg11", TAB_SCALES, [P, 2 * KP], U8))
         load_w1(0, 0, SLOT_C)
         v = {}
@@ -212,7 +212,7 @@ def tile_list_sauce_seasoning_kernel(
             if (g, rb) == (0, 1):
                 for c in range(2):
                     if u == 0:
-                        chunk_gate[c] = placed(f"gate_chunk{c}", (PICKS + 5.5, GATES + 4)[c], [P, 2, CH, 2], F32)
+                        chunk_gate[c] = placed(f"gate_chunk{c}", GATES + 4 + 2 * c, [P, 2, CH, 2], F32)
                     nc.scalar.activation(chunk_gate[c][:, u], pairs[:, c * CH : (c + 1) * CH, :], ACT.Sigmoid)
             else:
                 if u == 0:

@@ -237,14 +237,23 @@ def tile_list_sauce_seasoning_kernel(
                     **moving(a, first, width),
                 )
 
-        def features(g, rb, banks):
-            copied = placed(f"a_plain{g}{rb}", PAGE3 + 6 if g == 0 else PLAIN + 4 * (2 * g + rb), [P, 2, GR, 2], F32)
+        def feature_banks(g, rb, banks):
+            made = []
             for u in range(2):
                 bank = bank_tile(f"a{g}{rb}{u}", banks[u], [P, 2, GR])
                 for e in range(2):
                     feature_passes(bank[:, e, :], rb, 2 * u + e, g * GR, GR)
-                nc.scalar.copy(copied[:, u], bank[:].rearrange("p e j -> p j e"))
+                made.append(bank)
+            return made
+
+        def copy_features(g, rb, made, copied):
+            for u in range(2):
+                nc.scalar.copy(copied[:, u], made[u][:].rearrange("p e j -> p j e"))
             plain[g, rb] = copied
+
+        def features(g, rb, banks):
+            place = PAGE3 + 6 if g == 0 else PLAIN + 4 * (2 * g + rb)
+            copy_features(g, rb, feature_banks(g, rb, banks), placed(f"a_plain{g}{rb}", place, [P, 2, GR, 2], F32)[:])
 
         def chunk_features(rb, c, b):
             bank = bank_tile(f"a_chunk{rb}{c}", b, [P, PACK, CH])
@@ -396,50 +405,51 @@ def tile_list_sauce_seasoning_kernel(
         gate_features(1, 1, 1, 1)
         gate_features(1, 0)
         features(2, 0, (0, 1))
+        parked = feature_banks(2, 1, (6, 7))
         pick_intensity(2, kib=PICKS + 9)
         seasoning(0, 0, 2, 4)
         seasoning(0, 2, 2, 5)
-        square_intensity(2, 0, 4, 4)
         pick_intensity(3, 0, 2, QUARTER3)
         pick_intensity(3, 2, 6, PICKS + 13)
         late_pick = turn_pick(3, 0, 2, 1)
         quantize_h(1, plane_kib=QUARTER3 + 0.25)
         new = roots("roots_a", QUARTER3 - 2.75, 3)
-        replace(0, 0, 2, 6, new[0])
+        replace(0, 0, 2, 2, new[0])
         square_pick(*late_pick)
         replace(1, 0, 2, 1, new[1])
         replace(3, 0, 2, 0, new[2])
-        replace(2, 0, 2, 6, roots("root_b", QUARTER3 + 0.75, 1)[0])
-        features(2, 1, (1, 0))
+        copy_features(2, 1, parked, placed("a_plain_late", QUARTER3 + 0.75, [P, 2, GR, 2], F32)[:])
+        square_intensity(2, 0, 4, 2)
+        replace(2, 0, 2, 2, roots("root_b", PLAIN + 3, 1)[0])
         gate_group(2)
-        seasoning(1, 0, 2, 6)
-        seasoning(1, 2, 2, 1)
-        quantize_h(2, plane_kib=QUARTER3 + 1.5)
+        features(3, 0, (6, 7))
+        seasoning(1, 0, 2, 1)
+        seasoning(1, 2, 2, 0)
+        quantize_h(2, plane_kib=PLAIN + 3.5)
         new = roots("roots_c", QUARTER3 - 5.5, 3)
-        replace(0, 2, 2, 2, new[0])
-        square_intensity(3, 2, 2, 0)
-        replace(1, 2, 2, 3, new[1])
-        features(3, 0, (6, 1))
-        replace(2, 2, 2, 4, new[2])
-        replace(3, 2, 2, 5, roots("root_d", QUARTER3, 1)[0])
-        features(3, 1, (0, 6))
+        replace(0, 2, 2, 3, new[0])
+        square_intensity(3, 2, 2, 2)
+        replace(1, 2, 2, 4, new[1])
+        features(3, 1, (1, 0))
+        replace(2, 2, 2, 6, new[2])
+        replace(3, 2, 2, 5, roots("root_d", QUARTER3 - 0.25, 1)[0])
         gate_group(3)
-        square_intensity(0, 4, 4, 1)
-        square_intensity(1, 4, 4, 0)
-        seasoning(2, 0, 2, 6)
-        square_intensity(2, 4, 4, 2)
-        seasoning(2, 2, 2, 1)
-        square_intensity(3, 4, 4, 3)
-        quantize_h(3, plane_kib=QUARTER3 + 0.75)
+        square_intensity(0, 4, 4, 2)
+        square_intensity(1, 4, 4, 1)
+        seasoning(2, 0, 2, 0)
+        square_intensity(2, 4, 4, 3)
+        seasoning(2, 2, 2, 2)
+        square_intensity(3, 4, 4, 4)
+        quantize_h(3, plane_kib=QUARTER3 + 0.25)
         new = roots("roots_e", QUARTER3 - 8.25, 3)
         for nt in range(3):
-            replace(nt, 4, 2, (4, 5, 7)[nt], new[nt])
-        seasoning(3, 0, 2, 4)
-        seasoning(3, 2, 2, 5)
-        new = roots("roots_f", QUARTER3 + 3, 3)
+            replace(nt, 4, 2, (5, 6, 7)[nt], new[nt])
+        seasoning(3, 0, 2, 5)
+        seasoning(3, 2, 2, 6)
+        new = roots("roots_f", QUARTER3 + 5, 3)
         for nt in range(3):
             replace(nt, 6, 2, nt, new[nt])
             store(nt)
-        last = placed("root_last", QUARTER3 + 6, [P, 2 * GR], F32)
-        replace(3, 4, 4, 6, last[:])
+        last = placed("root_last", PLAIN + 20, [P, 2 * GR], F32)
+        replace(3, 4, 4, 3, last[:])
         store(3)

from contextlib import ExitStack

import concourse.mybir as mybir
from concourse.masks import make_identity

K, T, S, H, N = 1024, 2048, 1024, 1024, 512
FLOPS = 2 * (2 * K * H * S + H * N * S)

F32 = mybir.dt.float32
BF16 = mybir.dt.bfloat16
I32 = mybir.dt.int32
U32 = mybir.dt.uint32
U16 = mybir.dt.uint16
U8 = mybir.dt.uint8
FP8X4 = mybir.dt.float8_e4m3fn_x4
FP4X4 = mybir.dt.float4_e2m1fn_x4
ACT = mybir.ActivationFunctionType
ALU = mybir.AluOpType

P = 128
PACK = 4
KP = P * PACK
CH = 128
GR = 2 * CH
KIB = 1024

SLOT_A, IDENT, SLOT_B, SLOT_C = 0, 8.5, 9, 17
ROUNDED = (25.5, 72, 33.5, 38.5)
WO_SCALES, PAGE2, H_ROWS, WO_WORDS, PAGE3 = SLOT_C, SLOT_C + 0.5, 34, 42, 184
GATES, PLAIN, Y_SQ, G_SQ, PICKS = 50, 82, 114, 130, 146
QUARTER3, TAB_SCALES = 172, 180


def tile_list_sauce_seasoning_kernel(
    tc, tab_words, tab_scales, offs, w1, wg_words, wg_scales, wo_words, wo_scales, gT, out
):
    nc = tc.nc
    with ExitStack() as ctx:
        keep = ctx.enter_context(tc.tile_pool(name="keep", bufs=1))
        shared = ctx.enter_context(tc.tile_pool(name="shared", bufs=1))
        psum = ctx.enter_context(tc.psum_pool(name="psum", bufs=1))

        def kept(name, shape, dtype):
            return keep.tile(shape, dtype, name=name, align_bytes=64)

        def placed(name, kib, shape, dtype):
            return shared.tile(shape, dtype, name=name, offset=int(kib * KIB), align_bytes=64)

        def bank_tile(name, bank, shape):
            return psum.tile(shape, F32, name=name, offset=bank * 2 * KIB)

        offsets = keep.tile([P, S // 16], U16, name="offsets")
        nc.sync.dma_start(offsets[:], offs)

        def listed(first, count):
            return offsets[:, first * (CH // 16) : (first + count) * (CH // 16)]

        wg_sc_raw = placed("wg_sc_raw", SLOT_B - 0.25, [P, KP], U8)
        nc.sync.dma_start(wg_sc_raw[0:64, :].bitcast(I32), wg_scales.rearrange("a g (b c) -> (g b) a c", b=2).bitcast(I32))
        tab_sc = placed("tab_sc", TAB_SCALES, [P, T], U8)
        nc.sync.dma_start(tab_sc[64:96, :].bitcast(I32), tab_scales.rearrange("a g t -> g a t").bitcast(I32))
        wg_raw = placed("wg_raw", SLOT_C, [P, 2, 2 * H], U8)
        nc.sync.dma_start(wg_raw[:].bitcast(I32), wg_words.rearrange("a p b -> p a b").bitcast(I32))
        nc.vector.memset(wg_sc_raw[64:P, :].bitcast(I32), 0)
        nc.vector.memset(tab_sc[0:64, :].bitcast(I32), 0)
        nc.vector.memset(tab_sc[96:P, :].bitcast(I32), 0)
        wg_sc = kept("wg_sc", [P, 2 * H], U8)

        tab, w1_raw, page = {}, {}, {}

        def load_words(a, kib):
            words = placed(f"tab{a}", kib, [P, T], I32)
            nc.sync.dma_start(words[:], tab_words[a].rearrange("p t i -> p (t i)").bitcast(I32))
            tab[a] = words

        def load_w1(rb, a, kib):
            raw = placed(f"w1_raw{rb}{a}", kib, [P, PACK, KP], F32)
            nc.sync.dma_start(
                raw[:],
                w1[a * KP : (a + 1) * KP, rb * KP : (rb + 1) * KP].rearrange("(p j) c -> p j c", j=PACK),
            )
            w1_raw[rb, a] = raw

        def load_page(nt, kib):
            rows = placed(f"page{nt}", kib, [P, T], F32)
            nc.sync.dma_start(rows[:], gT[nt * P : (nt + 1) * P, :])
            page[nt] = rows

        load_words(0, SLOT_A)
        table_warm = kept("table_warm", [P, 1], F32)
        nc.gpsimd.memset(table_warm[:], 0.0)
        nc.scalar.activation(table_warm[:], table_warm[:], ACT.Sigmoid)

        wg_sc_dealt = kept("wg_sc_dealt", [P, KP], U8)
        nc.vector.tensor_copy(
            wg_sc_dealt[:].rearrange("p (t m) -> p t m", t=PACK), wg_sc_raw[:].rearrange("p (m t) -> p t m", t=PACK)
        )
        for q in range(4):
            nc.sync.dma_start(wg_sc[32 * q : 32 * q + 4, :].bitcast(I32), wg_sc_dealt[16 * q : 16 * q + 16, :].bitcast(I32))
        load_words(1, SLOT_B)
        ident = placed("ident", IDENT, [P, P], F32)
        make_identity(nc, ident[:])
        wg = {}

        def order_wg(rb, first, count, block):
            nc.scalar.copy(
                block[:].bitcast(U16).rearrange("p (a t m) -> p a t m", a=count, t=PACK),
                wg_raw[:]
                .bitcast(U16)[:, first : first + count, rb * KP : (rb + 1) * KP]
                .rearrange("p a (m t) -> p a t m", t=PACK),
            )
            for i in range(count):
                wg[rb, first + i] = block[:, i * 2 * KP : (i + 1) * 2 * KP]

        order_wg(0, 0, 2, kept("wg0", [P, 2 * 2 * KP], U8))
        order_wg(1, 0, 1, kept("wg10", [P, 2 * KP], U8))
        v_sc_picked = kept("v_sc_picked", [P, S], U8)
        nc.vector.tensor_copy(v_sc_picked[:], tab_sc[:].indirect(offsets[:]))
        v_sc = kept("v_sc", [P, 2 * S], U8)
        for q in range(4):
            nc.sync.dma_start(v_sc[32 * q : 32 * q + 4, :].bitcast(I32), v_sc_picked[64 + 8 * q : 72 + 8 * q, :].bitcast(I32))
        order_wg(1, 1, 1, placed("wg11", TAB_SCALES, [P, 2 * KP], U8))
        load_w1(0, 0, SLOT_C)
        v = {}
        for a in range(2):
            for first, count in ((0, 2), (2, 2), (4, 4)):
                words = kept(f"v{a}{first}", [P, count * CH], U32)
                nc.vector.tensor_copy(words[:], tab[a][:].bitcast(U32).indirect(listed(first, count)))
                for i in range(count // 2):
                    v[a, first // 2 + i] = words[:, i * GR : (i + 1) * GR]
            load_w1(a, 1 - a, (SLOT_A, SLOT_B)[a])

        def quantize(name, src, width, kib=None, plane_kib=None):
            if kib is None:
                codes = kept(f"{name}_codes", [P, width], U32)
            else:
                codes = placed(f"{name}_codes", kib, [P, width], U32)
            if plane_kib is None:
                scales = kept(f"{name}_scales", [P, width], U8)
            else:
                scales = placed(f"{name}_scales", plane_kib, [P, width], U8)
            nc.vector.quantize_mx(out=codes[:].bitcast(FP8X4), scales=scales[:], in_=src)
            return [(codes[:, i : i + P], scales[:, i : i + P]) for i in range(0, width, P)]

        w1_bf, w1q = {}, {}

        def round_w1(rb, a):
            grouped = placed(f"w1_bf{rb}{a}", ROUNDED[2 * rb + a], [P, PACK * KP], BF16)
            nc.vector.tensor_copy(
                grouped[:].rearrange("p (t m e j) -> p m j e t", t=PACK, e=2, j=PACK),
                w1_raw[rb, a][:].rearrange("p j (m e t) -> p m j e t", e=2, t=PACK),
            )
            w1_bf[rb, a] = grouped[:]

        def quantize_w1(rb, a):
            w1q[rb, a] = quantize(f"w1q{rb}{a}", w1_bf[rb, a], KP)

        round_w1(0, 0)
        load_w1(1, 1, SLOT_C)
        quantize_w1(0, 0)
        round_w1(0, 1)
        load_page(0, SLOT_A)
        quantize_w1(0, 1)
        round_w1(1, 0)
        load_page(1, SLOT_B)
        quantize_w1(1, 0)
        round_w1(1, 1)
        load_page(2, PAGE2)
        wo_sc = placed("wo_sc", WO_SCALES, [P, N], U8)
        for q in range(4):
            nc.sync.dma_start(
                wo_sc[32 * q : 32 * q + 8, :].bitcast(I32), wo_scales[:, 4 * q : 4 * q + 4, :].bitcast(I32)
            )
        quantize_w1(1, 1)
        wo = {}

        def load_wo(pair, kib):
            words = placed(f"wo{pair}", kib, [P, 2, GR], I32)
            nc.sync.dma_start(
                words[:], wo_words[:, :, pair * GR : (pair + 1) * GR, :].rearrange("a p c i -> p a (c i)").bitcast(I32)
            )
            wo[pair] = words

        load_wo(0, WO_WORDS)

        logits, gate, chunk_gate, plain, hq, h_rows = {}, {}, {}, {}, {}, {}

        def moving(a, first, width):
            col = first % GR
            return {
                "rhs": v[a, first // GR][:, col : col + width].bitcast(FP8X4),
                "rhs_scale": v_sc[:, a * S + first : a * S + first + width],
            }

        def gate_pass(g, rb, u, a, opens):
            if opens:
                logits[g, rb, u] = bank_tile(f"b{g}{rb}{u}", 4 * rb + 2 * (g % 2) + u, [P, 2, GR])
            for e in range(2):
                t = 2 * u + e
                col = rb * H + a * KP + t * P
                nc.tensor.matmul_mx(
                    out=logits[g, rb, u][:, e, :],
                    lhsT=wg[rb, a][:, 2 * t * P : 2 * (t + 1) * P].bitcast(FP4X4),
                    lhsT_scale=wg_sc[:, col : col + P],
                    start=(opens and e == 0),
                    stop=(not opens and e == 1),
                    **moving(a, g * GR, GR),
                )

        def sigmoid(g, rb, u):
            pairs = logits[g, rb, u][:].rearrange("p e j -> p j e")
            if (g, rb) == (0, 1):
                for c in range(2):
                    if u == 0:
                        chunk_gate[c] = placed(f"gate_chunk{c}", GATES + 4 + 2 * c, [P, 2, CH, 2], F32)
                    nc.scalar.activation(chunk_gate[c][:, u], pairs[:, c * CH : (c + 1) * CH, :], ACT.Sigmoid)
            else:
                if u == 0:
                    gate[g, rb] = placed(f"gate{g}{rb}", GATES + 4 * (2 * g + rb), [P, 2, GR, 2], F32)
                nc.scalar.activation(gate[g, rb][:, u], pairs, ACT.Sigmoid)

        def gates(g, rb):
            for u in range(2):
                gate_pass(g, rb, u, 1, True)
                gate_pass(g, rb, u, 0, False)
                sigmoid(g, rb, u)

        def feature_passes(dst, rb, t, first, width):
            for a in range(2):
                wc, ws = w1q[rb, a][t]
                nc.tensor.matmul_mx(
                    out=dst,
                    lhsT=wc.bitcast(FP8X4),
                    lhsT_scale=ws,
                    start=(a == 0),
                    stop=(a == 1),
                    **moving(a, first, width),
                )

        def feature_banks(g, rb, banks):
            made = []
            for u in range(2):
                bank = bank_tile(f"a{g}{rb}{u}", banks[u], [P, 2, GR])
                for e in range(2):
                    feature_passes(bank[:, e, :], rb, 2 * u + e, g * GR, GR)
                made.append(bank)
            return made

        def copy_features(g, rb, made, copied):
            for u in range(2):
                nc.scalar.copy(copied[:, u], made[u][:].rearrange("p e j -> p j e"))
            plain[g, rb] = copied

        def features(g, rb, banks):
            place = PAGE3 + 6 if g == 0 else PLAIN + 4 * (2 * g + rb)
            copy_features(g, rb, feature_banks(g, rb, banks), placed(f"a_plain{g}{rb}", place, [P, 2, GR, 2], F32)[:])

        def chunk_features(rb, c, b):
            bank = bank_tile(f"a_chunk{rb}{c}", b, [P, PACK, CH])
            for t in range(PACK):
                feature_passes(bank[:, t, :], rb, t, c * CH, CH)
            return bank

        h_space = placed("h_bf", H_ROWS, [P, 5 * KP], BF16)

        def open_h(g):
            start = KP if g == 0 else 0
            h_rows[g] = h_space[:, start : start + 4 * KP].rearrange("p (r j u e) -> p r j u e", r=2, u=2, e=2)

        def block_place(g, rb):
            return 1 - rb if g == 1 else rb

        def gate_features(g, rb, first=0, count=2):
            cols = slice(first * CH, (first + count) * CH)
            nc.gpsimd.tensor_tensor(
                h_rows[g][:, block_place(g, rb), cols],
                plain[g, rb][:, :, cols, :].rearrange("p u j e -> p j u e"),
                gate[g, rb][:, :, cols, :].rearrange("p u j e -> p j u e"),
                ALU.mult,
            )

        def gate_chunk(engine, c, sums):
            engine.tensor_tensor(
                h_rows[0][:, 1, c * CH : (c + 1) * CH],
                sums,
                chunk_gate[c][:].rearrange("p u j e -> p j u e"),
                ALU.mult,
            )

        def gate_group(g):
            open_h(g)
            gate_features(g, 0)
            gate_features(g, 1)

        y_sq, g_pick, g_sq = {}, {}, {}

        def quantize_h(g, kib=None, plane_kib=None):
            made = quantize(f"hq{g}", h_rows[g].rearrange("p r j u e -> p (r j u e)"), 2 * GR, kib, plane_kib)
            for i, operand in enumerate(made):
                hq[block_place(g, i // 2), 2 * g + i % 2] = operand

        def seasoning(g, first, count, b):
            cols = slice(first * P, (first + count) * P)
            bank = bank_tile(f"y{g}{first}", b, [P, 2, count * P])
            for i in range(2):
                for rb in range(2):
                    codes, scales = hq[rb, 2 * g + i]
                    nc.tensor.matmul_mx(
                        out=bank[:, i, :],
                        lhsT=codes.bitcast(FP8X4),
                        lhsT_scale=scales,
                        rhs=wo[first // 2][:, rb, :].bitcast(FP8X4),
                        rhs_scale=wo_sc[4 * rb : P, cols],
                        start=(rb == 0),
                        stop=(rb == 1),
                    )
            for k in range(count):
                nt = first + k
                sq = placed(f"y_sq{g}{nt}", Y_SQ + 4 * g + nt, [P, 2, P], F32)
                nc.scalar.activation(sq[:], bank[:, :, k * P : (k + 1) * P], ACT.Square)
                for i in range(2):
                    y_sq[2 * g + i, nt] = sq[:, i, :]

        def pick_intensity(nt, first=0, count=8, kib=None):
            place = PICKS + 4 * nt + first / 2 if kib is None else kib
            picked = placed(f"g_pick{nt}{first}", place, [P, count * CH], F32)
            nc.vector.tensor_copy(picked[:], page[nt][:].indirect(listed(first, count)))
            for i in range(count):
                g_pick[nt, first + i] = picked[:, i * CH : (i + 1) * CH]

        def turn_pick(nt, first, count, b):
            bank = bank_tile(f"g{nt}{first}", b, [P, count, P])
            for i in range(count):
                nc.tensor.transpose(bank[:, i, :], g_pick[nt, first + i], ident[:])
            return nt, first, count, bank

        def square_pick(nt, first, count, bank):
            sq = placed(f"g_sq{nt}{first}", G_SQ + 4 * nt + first / 2, [P, count, P], F32)
            nc.scalar.activation(sq[:], bank[:], ACT.Square)
            for i in range(count):
                g_sq[nt, first + i] = sq[:, i, :]

        def square_intensity(nt, first, count, b):
            square_pick(*turn_pick(nt, first, count, b))

        def roots(name, kib, count):
            rows = placed(name, kib, [P, count, GR], F32)
            return [rows[:, i, :] for i in range(count)]

        def open_sum(nt, first, count, b):
            bank = bank_tile(f"sum{nt}{first}", b, [P, count, CH])
            picked = [g_sq[nt, c] for c in range(first, first + count)]
            made = [y_sq[c, nt] for c in range(first, first + count)]
            terms = picked + made if nt + first == 0 else made + picked
            for i, term in enumerate(terms):
                nc.tensor.matmul(
                    bank[:, i % count, :], term, ident[:], start=(i == 0), stop=(i == 2 * count - 1), is_transpose=True
                )
            return nt, first, count, bank

        def scatter_root(nt, first, count, bank, new):
            nc.scalar.activation(new, bank[:].rearrange("p i j -> p (i j)"), ACT.Sqrt)
            nc.vector.tensor_copy(page[nt][:].indirect(listed(first, count)), new)

        def replace(nt, first, count, b, new):
            scatter_root(*open_sum(nt, first, count, b), new)

        def store(nt):
            nc.sync.dma_start(out[nt * P : (nt + 1) * P, :], page[nt][:])

        for u in range(2):
            gate_pass(0, 0, u, 0, True)
        for u in range(2):
            gate_pass(0, 0, u, 1, False)
            sigmoid(0, 0, u)
        gates(0, 1)
        gates(1, 0)
        gates(1, 1)
        gates(2, 0)
        features(0, 0, (0, 1))
        gates(3, 1)
        gates(3, 0)
        gates(2, 1)
        direct = [chunk_features(1, c, 6 + c) for c in range(2)]
        chunk_plain = placed("a_chunk", PLAIN, [P, CH, 2, 2], F32)
        nc.scalar.copy(chunk_plain[:], direct[1][:].rearrange("p (u e) j -> p j u e", e=2))
        features(1, 1, (0, 1))
        root_warm = kept("root_warm", [P, 1], F32)
        nc.scalar.activation(root_warm[:], plain[1, 1][:, 1, 0, 0:1], ACT.Sqrt, scale=0.0, bias=gate[2, 1][:, 1, 0, 0:1])
        pick_intensity(0)
        open_h(0)
        gate_features(0, 0)
        load_page(3, PAGE3)
        load_wo(1, PAGE3 + 8)
        gate_chunk(nc.vector, 0, direct[0][:].rearrange("p (u e) j -> p j u e", e=2))
        gate_chunk(nc.gpsimd, 1, chunk_plain[:])
        open_h(1)
        gate_features(1, 1, 0, 1)
        features(1, 0, (0, 1))
        square_intensity(0, 0, 4, 6)
        pick_intensity(1, 0, 4, PICKS + 4.5)
        pick_intensity(1, 4, 4, PICKS + 6.5)
        square_intensity(1, 0, 4, 7)
        quantize_h(0, plane_kib=PICKS + 4.25)
        gate_features(1, 1, 1, 1)
        gate_features(1, 0)
        features(2, 0, (0, 1))
        parked = feature_banks(2, 1, (6, 7))
        pick_intensity(2, kib=PICKS + 9)
        seasoning(0, 0, 2, 4)
        seasoning(0, 2, 2, 5)
        pick_intensity(3, 0, 2, QUARTER3)
        pick_intensity(3, 2, 6, PICKS + 13)
        late_pick = turn_pick(3, 0, 2, 1)
        quantize_h(1, plane_kib=QUARTER3 + 0.25)
        new = roots("roots_a", QUARTER3 - 2.75, 3)
        replace(0, 0, 2, 2, new[0])
        square_pick(*late_pick)
        replace(1, 0, 2, 1, new[1])
        replace(3, 0, 2, 0, new[2])
        copy_features(2, 1, parked, placed("a_plain_late", QUARTER3 + 0.75, [P, 2, GR, 2], F32)[:])
        square_intensity(2, 0, 4, 2)
        replace(2, 0, 2, 2, roots("root_b", PLAIN + 3, 1)[0])
        gate_group(2)
        features(3, 0, (6, 7))
        seasoning(1, 0, 2, 1)
        seasoning(1, 2, 2, 0)
        quantize_h(2, plane_kib=PLAIN + 3.5)
        new = roots("roots_c", QUARTER3 - 5.5, 3)
        replace(0, 2, 2, 3, new[0])
        square_intensity(3, 2, 2, 2)
        replace(1, 2, 2, 4, new[1])
        features(3, 1, (1, 0))
        replace(2, 2, 2, 6, new[2])
        replace(3, 2, 2, 5, roots("root_d", QUARTER3 - 0.25, 1)[0])
        gate_group(3)
        square_intensity(0, 4, 4, 2)
        square_intensity(1, 4, 4, 1)
        seasoning(2, 0, 2, 0)
        square_intensity(2, 4, 4, 3)
        seasoning(2, 2, 2, 2)
        square_intensity(3, 4, 4, 4)
        quantize_h(3, plane_kib=QUARTER3 + 0.25)
        new = roots("roots_e", QUARTER3 - 8.25, 3)
        for nt in range(3):
            replace(nt, 4, 2, (5, 6, 7)[nt], new[nt])
        seasoning(3, 0, 2, 5)
        seasoning(3, 2, 2, 6)
        new = roots("roots_f", QUARTER3 + 5, 3)
        for nt in range(3):
            replace(nt, 6, 2, nt, new[nt])
            store(nt)
        last = placed("root_last", PLAIN + 20, [P, 2 * GR], F32)
        replace(3, 4, 4, 3, last[:])
        store(3)
